import numpy as np, ml_dtypes
CORES = [16,17,18,19,32,33,34,35]
N = 8
BF = ml_dtypes.bfloat16
def gentries(a):
    return np.ascontiguousarray(a.reshape(8, 16, -1).transpose(0, 2, 1)).reshape(8, -1)
def gtable(e):
    e = np.asarray(e); return np.ascontiguousarray(e.reshape(8, -1, 16).transpose(0, 2, 1)).reshape(128, -1).astype(np.int32)
V, Q, T, S, HOP = 2048, 256, 2, 2, 3
TH, TAU = 1020, (1020, 1530)
def toward(rng, shape, hub, share):
    h = hub[np.arange(8).reshape((1, 8) + (1,) * (len(shape) - 2)), rng.integers(0, hub.shape[1], shape)]
    return np.where(rng.random(shape) < share, h, rng.integers(0, V, shape))
def parts(rng):
    hub = rng.integers(0, V, (8, 32))
    X = rng.integers(0, 256, (N, 8, 16, V)); E = toward(rng, (N, 8, 16, V), hub, 0.1)
    v = toward(rng, (N, 8, Q), hub, 0.2); z = rng.integers(0, 256, (N, 8, 16, Q)); L = toward(rng, (N, 8, 16, Q), hub, 0.3)
    return X, E, v, z, L
def pack(X, E, v, z, L):
    return {"X": np.ascontiguousarray(X.reshape(N, 128, V)).astype(np.float32).astype(BF), "E": np.ascontiguousarray(E.reshape(N, 128, V)).astype(np.int32),
            "v0": np.stack([gtable(a) for a in v]), "z0": np.ascontiguousarray(z.reshape(N, 128, Q)).astype(np.float32).astype(BF), "L0": np.ascontiguousarray(L.reshape(N, 128, Q)).astype(np.int32)}
def setup_inputs(rng):
    return pack(*parts(rng))
def skew(rng, shape):
    col = shape[:2] + (1, shape[3])
    x = np.minimum((np.exp2(8 * rng.random(col)) * rng.random(shape)).astype(np.int64), 255)
    return np.where(rng.random(shape) < 0.5 * rng.integers(0, 2, col), 255 - x, x)
def lean(rng, shape):
    u = rng.random(shape); i = np.minimum((V * u * u * u).astype(np.int64), V - 1)
    return np.where(rng.random(shape[:2] + (1,) * (len(shape) - 2)) < 0.5, V - 1 - i, i)
def setup_inputs_spread(rng):
    return pack(skew(rng, (N, 8, 16, V)), lean(rng, (N, 8, 16, V)), lean(rng, (N, 8, Q)), skew(rng, (N, 8, 16, Q)), lean(rng, (N, 8, 16, Q)))
def setup_inputs_ends(rng):
    X, E, v, z, L = parts(rng)
    X = 255 * (rng.random(X.shape) < rng.choice(np.array([0.1, 0.5, 0.9]), (N, 8, 1, V))).astype(np.int64)
    z = 255 * (rng.random(z.shape) < rng.choice(np.array([0.0, 0.25, 0.5, 0.75, 1.0]), (N, 8, 1, Q))).astype(np.int64)
    E, v, L = [np.where(rng.random(a.shape) < 0.75, (V - 1) * rng.integers(0, 2, a.shape), a) for a in (E, v, L)]
    X[..., [0, 1, V - 3]] = 0; X[..., [2, V - 2, V - 1]] = 255
    for g in range(8):
        tie, full = (V - 1, V - 2) if g % 2 == 0 else (V - 2, V - 1)
        E[:, g, :, tie] = np.array([2, V - 1, V - 2, V - 1] * 4); E[:, g, :, full] = V - 1
        E[:, g, :, 1] = np.array([V - 3, 0, 1, 0] * 4); E[:, g, :, V - 3] = 0; E[:, g, :, 2] = np.array([V - 1, 2] * 8)
        if g % 4 != 2: E[:, g, 0, 0] = V - 1; E[:, g, 1, 0] = 0
    v[..., Q - 1] = V - 1; v[..., Q - 2] = V - 2; z[..., Q - 2:] = 0; L[..., Q - 2:] = V - 1; L[:, :, 15, Q - 2:] = 0
    v[..., 0] = 1; z[..., 0] = 255; v[..., 1] = 1; z[..., 1] = 0
    return pack(X, E, v, z, L)
def setup_inputs_corners(rng):
    X, E, v, z, L = parts(rng); own = np.arange(V); kinds = rng.permutation(8); h = V // 2
    for g in range(8):
        e, l, k = E[:, g], L[:, g], int(kinds[g])
        if k == 0: e[:] = own
        elif k == 1: e[:, 0::2] = (own + 1) % V; e[:, 1::2] = (own - 1) % V
        elif k == 2: e[:] = 0; e[:, 0] = V - 1
        elif k == 3:
            w = int(rng.choice(np.array([0, V - 1, h]))); l[:] = w; z[:, g] = 0
            e[:, 1] = e[:, 0]
            e[:, 0::2, w] = 5; e[:, 1::2, w] = 6; X[:, g, :, 5] = 255; X[:, g, :, 6] = 0
        elif k == 4: v[:, g] = V - 1; l[:] = V - 1
        elif k == 5:
            few = rng.permutation(h)[:64]; x = X[:, g]; x[:] = rng.integers(70, 256, x.shape)
            x[:, :, few[:32]] = rng.integers(240, 256, (N, 16, 32)); x[:, :, few[32:]] = rng.integers(70, 81, (N, 16, 32))
            e[:] = rng.integers(0, h, e.shape); e[:, 1, :h] = e[:, 0, :h]; z[:, g] = 0
            e[:, 0, h:] = few[rng.integers(0, 32, (N, V - h))]; e[:, 1, h:] = few[rng.integers(32, 64, (N, V - h))]
            l[:, :15] = rng.integers(0, h, (N, 15, Q)); l[:, 15] = rng.integers(h, V, (N, Q))
        elif k == 6: z[:, g] = 255; z[int(rng.integers(0, N)), g] = 0
        else:
            c = V // 4; o = rng.permutation(V).reshape(4, c); x = X[:, g]; z[:, g] = 255
            for i in range(4): e[:, :, o[i]] = o[i][rng.integers(0, c, (N, 16, c))]
            x[:, :, o[0]] = rng.integers(0, 64, (N, 16, c))
            x[:, :, o[1]] = rng.integers(252, 256, (N, 16, c)); x[:, :5, o[1]] = rng.integers(0, 16, (N, 5, c))
            x[:, :, o[2]] = np.array([0] * 5 + [255] * 2 + [215] * 2 + [255] * 7)[:, None]
            x[:, :, o[3]] = np.array([0] * 4 + [254] + [255] * 11)[:, None]
    v[..., 0] = 0; v[..., Q - 1] = V - 1
    return pack(X, E, v, z, L)
def setup_inputs_crowd(rng):
    X, E, v, z, L = parts(rng); A = T * S
    kinds = np.stack([rng.permutation(np.array([0, 1, 2, 4])), rng.permutation(np.array([0, 1, 3, 4]))], axis=1).reshape(-1)
    for g in range(8):
        k = int(kinds[g])
        if k == 4: continue
        h = V // 2; four = np.array([0, V - 1, 1 + 2 * int(rng.integers(0, V // 4)), h + 2 * int(rng.integers(0, V // 4))])
        o = rng.permutation(np.setdiff1d(np.arange(V), four))
        hi = np.concatenate([four, o[:h - 4]]); lo = o[h - 4:]
        w = X[:, g]; w[:, :, hi] = rng.integers(240, 256, (N, 16, h)); w[:, :, lo] = rng.integers(70, 81, (N, 16, h))
        z[:, g] = rng.integers(0, 4, (N, 16, Q))
        e = E[:, g]; e[:, :2] = lo[rng.integers(0, h, (N, 2, V))]
        if k < 2:
            hs = hi[:4]; names = np.repeat(hs[(np.arange(N) + int(rng.integers(0, 4))) % 4][:, None], Q, axis=1)
            if k == 1:
                miss = rng.integers(0, Q, N); miss[int(rng.integers(0, N))] = Q - 1; names[np.arange(N), miss] = -1
        elif k == 2:
            hs = hi[:4]; names = rng.choice(hs, (N, Q))
        else:
            hs = hi[rng.permutation(h)[:Q]]; names = np.stack([rng.permutation(hs) for _ in range(N)])
        n = len(hs)
        a = e[:, 0::2]; a[:, :, hs] = hi[rng.integers(4 if k < 2 else 0, h, (N, 8, n))]
        b = e[:, 1::2]; b[:, :, hs] = lo[rng.integers(0, h, (N, 8, n))]
        l = lo[rng.integers(0, h, (N, 16, Q))]
        here = np.argsort(np.argsort(rng.random((N, 16 - A, Q)), axis=1), axis=1) < T
        l[:, A:] = np.where(here & (names >= 0)[:, None], names[:, None], l[:, A:])
        L[:, g] = l
    return pack(X, E, v, z, L)
def setup_inputs_ties(rng):
    X, E, v, z, L = parts(rng); h = V // 2; o = rng.permutation(V); tw = np.zeros(V, np.int64); tw[o[:h]] = o[h:]; tw[o[h:]] = o[:h]
    X = 51 * rng.integers(0, 6, X.shape); z = 51 * rng.integers(0, 6, z.shape); X[..., o[:h]] = X[..., o[h:]]
    E[:, :, 8:] = tw[E[:, :, :8]]; E = np.ascontiguousarray(E[:, :, rng.permutation(16)])
    X[..., V - 2] = 0; X[:, :, 12:, V - 2] = 255; X[..., V - 4] = 0
    E[..., V - 1] = V - 2; E[..., V - 2] = V - 2; E[..., V - 3] = V - 4; E[:, :, 0, V - 3] = V - 2
    v[..., Q - 2:] = V - 1; z[..., Q - 2:] = 0; z[:, :, 0, Q - 2] = 51; L[..., Q - 2:] = V - 3
    return pack(X, E, v, z, L)
def check_inputs(d):
    bad = []
    for k, lo, hi in (("X", 0, 255), ("E", 0, V - 1), ("v0", 0, V - 1), ("z0", 0, 255), ("L0", 0, V - 1)):
        a = np.asarray(d[k]).astype(np.float64)
        if not (np.min(a) >= lo and np.max(a) <= hi and np.all(a == np.floor(a))): bad.append("range of " + k)
    return bad
def pick(tab, ix):
    return np.take_along_axis(tab, ix[:, None, :], 2)
def reference(X, E, v0, z0, L0):
    x = X.astype(np.float32).astype(np.int64).reshape(N, 8, 16, V); e = E.astype(np.int64).reshape(N, 8, 16, V)
    v = np.stack([gentries(a) for a in v0]).astype(np.int64)
    z = z0.astype(np.float32).astype(np.int64).reshape(N, 8, 16, Q); L = L0.astype(np.int64).reshape(N, 8, 16, Q)
    wt = (2 * np.arange(16) + 1)[None, :, None]
    for t in range(T):
        mark = np.zeros((N, 8, V), bool)
        for r in range(N):
            p = (r + HOP * t) % N; s = (p + HOP) % N; zr = z[r].copy(); vr = v[r].copy(); ll = L[r].copy()
            for step in range(S):
                c = pick(e[p], vr)
                far = np.add.reduce(np.abs(pick(x[p], c.reshape(8, -1)).reshape(8, 16, 16, Q) - zr[:, :, None, :]), axis=1)
                k = np.argmin(far, axis=1)
                vr = np.take_along_axis(c, k[:, None, :], 1)[:, 0]; ll[:, S * t + step] = vr
            like = np.min(far, axis=1) <= TH; xv = pick(x[p], vr)
            flat = ll.reshape(8, -1); a = np.take_along_axis(e[s][:, 0], flat, 1); b = np.take_along_axis(e[s][:, 1], flat, 1)
            zz = np.tile(zr, (1, 1, 16))
            gap = np.add.reduce(np.abs(np.maximum(pick(x[s], a), zz) - np.maximum(pick(x[s], b), zz)), axis=1).reshape(8, 16, Q)
            fail = gap > TAU[t]; some = np.any(fail, axis=1); f = np.argmax(fail, axis=1)
            cut = ~like & some; none = ~like & ~some
            u = np.take_along_axis(ll, f[:, None, :], 1)[:, 0]; base = np.take_along_axis(a.reshape(8, 16, Q), f[:, None, :], 1)[:, 0]
            gi, qi = np.nonzero(cut)
            mark[s, gi, u[gi, qi]] = True; ll[gi, f[gi, qi], qi] = base[gi, qi]
            half = (zr + xv) >> 1; h = np.add.reduce(half * wt, axis=1) & (V - 1)
            L[r] = ll; v[r] = np.where(cut, base, np.where(none, h, vr))
            z[r] = np.where(like[:, None, :], np.abs(zr - xv), np.where(none[:, None, :], half, zr))
        e = np.where(mark[:, :, None, :], np.roll(e, -1, axis=2), e)
    ya = np.add.reduce(e * (np.arange(16) + 1)[None, None, :, None], axis=2)
    return {"yv": v.astype(np.float32), "yz": z.reshape(N, 128, Q).astype(np.float32), "yl": L.reshape(N, 128, Q).astype(np.float32), "ya": ya.astype(np.float32)}

@@ -1,0 +1,635 @@
+import numpy as np
+from concourse.mybir import AluOpType as OP, AxisListType, ActivationFunctionType as AF
+
+F, B, I, U = "float32", "bfloat16", "int32", "uint16"
+SB = {
+    "eS": (2048, I), "xS": (2048, B), "zA": (256, B), "LA": (256, I), "vA": (16, I), "ef": (2048, F),
+    "t0": (128, I), "t1": (128, I), "t2": (128, I), "tf": (384, F), "elf": (384, F), "el": (256, U), "el2": (256, U),
+    "e0r": (128, I), "e1r": (128, I), "ys": (2048, F), "s0r": (128, F), "s1r": (128, F), "dy0": (128, F), "dy1": (128, F),
+    "iD": (256, I), "iA": (256, I), "iC": (8, I), "iN": (256, I), "zl": (256, U), "col": (32, F), "mg": (128, F),
+    "kk": (256, F), "io128": (128, B), "io16": (16, F), "jm": (16, F), "g16": (16, F), "gp": (16, F), "io2k": (2048, F),
+    "ck": (256, B), "ones": (128, B), "maskJ": (256, F), "Ib": (128, B), "nIb": (128, B), "If": (128, F), "PHI": (256, B),
+    "P16": (256, B), "W16": (16, B), "B8p": (8, B), "B8n": (8, B), "W8h": (8, B), "BB": (128, B), "BBf": (128, F),
+    "Sel0f": (128, F), "S8f": (8, F), "B8f": (8, F), "BW0": (128, B), "BW1": (128, B), "BD0": (128, F), "BD1": (128, F),
+    "BH": (2048, B), "IJ": (2048, B), "RST": (256, F), "RS01": (256, F), "WY": (16, F),
+    "XA": (2048, B), "XB": (2048, B), "HI": (2048, B), "LO": (2048, B), "MARK": (2048, B),
+    "zx0": (4096, B), "zx1": (4096, B), "df": (4096, B), "ab": (4096, B), "c16": (256, U), "cf": (256, F), "H": (256, B),
+    "mk": (256, B), "R": (512, F), "wi": (32, I), "wa": (32, I), "wb": (32, B), "wT": (128, B), "mj": (256, F),
+    "sc": (256, F), "vlA": (16, U), "v1o0": (16, U), "v2o0": (16, U), "v1o1": (16, U), "v2o1": (16, U), "xo0": (256, B),
+    "xo1": (256, B), "vlB": (16, U),
+    "sh": (1024, B), "sl": (1024, B), "mh": (4096, B), "ml": (4096, B), "eh": (512, B), "en": (512, B), "Lb": (256, F),
+    "r1": (256, F), "r2": (256, F), "v2n": (256, F), "KL": (256, F), "ab2": (256, B), "hf": (256, I), "hb": (256, B),
+    "like": (256, B), "tl": (256, B), "w": (256, B), "fk": (256, F), "fk2": (256, F), "R2": (256, F), "qs": (160, F),
+    "qi": (64, I), "kT": (128, F), "ui": (32, I), "ul": (16, U), "cutE": (256, B), "oh": (256, F), "ce": (256, F),
+    "ce2": (256, F), "smk": (256, F), "aK": (256, F), "e1": (256, F), "e2": (256, F), "KL2": (256, F), "OH": (4096, B),
+    "m0": (128, B), "m1": (128, B), "mi": (64, I), "mf": (64, F), "dl": (256, F), "dm": (256, F), "mlf": (128, F),
+    "Lo0": (256, U), "zo1": (256, B), "Lo1": (256, U), "zo2": (256, B), "Lo2": (256, U), "vo2": (16, F),
+    "zB": (256, B), "LB": (256, U), "v1i0": (16, U), "v2i0": (16, U), "xi0": (256, B), "zC": (256, B), "LC": (256, U),
+    "v1i1": (16, U), "v2i1": (16, U), "xi1": (256, B), "zF": (256, B), "LF": (256, U), "vF": (16, F),
+    "yzs": (256, F), "yls": (256, F), "yvs": (128, F), "yas": (128, F), "ya1": (128, F), "ya2": (128, F), "ya3": (128, F),
+    "ya4": (128, F), "ya5": (128, F),
+}
+PS = {"K0": 512, "K1": 512, "G": 512, "N0": 512, "N1": 512, "N2": 512, "Q0": 512, "Q1": 512}
+SCRATCH = {}
+PLACE = {}
+_use = {F: 0, B: 0, I: 0, U: 0}
+for _n, (_w, _d) in SB.items():
+    if _w > 600:
+        SCRATCH[_n] = ("sbuf", [128, _w], _d)
+        PLACE[_n] = (_n, 0)
+    else:
+        PLACE[_n] = ("all_" + _d, _use[_d])
+        _use[_d] += -(-_w // 32) * 32
+for _d in _use:
+    SCRATCH["all_" + _d] = ("sbuf", [128, _use[_d]], _d)
+for _n, _w in PS.items():
+    SCRATCH[_n] = ("psum", [128, _w], "float32")
+SEMAPHORES = ["cV", "cS", "cT", "cG"] + ["d%d" % i for i in range(30)] + ["a%d" % i for i in range(16)] + ["l%d" % i for i in range(16)]
+
+
+def rank_program(g, core, T, topo):
+    rank = T.rank_of(core)
+    if rank is None:
+        return
+    nR = len(T.cores)
+    HOP = 3
+    SHARE = 32
+    TH, TAU = 1020, (1020, 1530)
+    nxt, home = T.cores[(rank + HOP) % nR], T.cores[(rank - 2 * HOP) % nR]
+
+    QS = {"V": g.vector, "S": g.scalar, "T": g.tensor, "G": g, "Y": g.sync}
+    SEMQ = {"V": "cV", "S": "cS", "T": "cT", "G": "cG"}
+    count = {}
+    known = {q: {} for q in QS}
+    toks = []
+    hist = {}
+
+    def track(name):
+        if name not in hist:
+            hist[name] = {"w": np.full(SB[name][0] if name in SB else 1, -1), "r": {}}
+        return hist[name]
+
+    def cols(r):
+        return slice(0, 1) if r[0] in PS else slice(r[1], r[2], r[3])
+
+    def need(q, reads, writes):
+        ids = set()
+        for r in reads + writes:
+            h = track(r[0])
+            ps = r[0] in PS
+            new = set(int(i) for i in np.unique(h["w"][cols(r)]))
+            if ps or r in writes:
+                for k, arr in h["r"].items():
+                    if not (ps and k == q and r not in writes):
+                        new.update(int(i) for i in np.unique(arr[cols(r)]))
+            if ps and q == "T":
+                new = {i for i in new if i < 0 or toks[i][3] != "T"}
+            ids |= new
+        ids.discard(-1)
+        kn = known[q]
+        want = {}
+        for i in ids:
+            s, v = toks[i][0], toks[i][1]
+            if s[0] == "d":
+                v = count[s]
+            if kn.get(s, 0) < v:
+                want[s] = max(want.get(s, 0), v)
+        for s in list(want):
+            for i in ids:
+                s2 = toks[i][0]
+                if s2 != s and s2 in want and toks[i][2].get(s, 0) >= want[s] and toks[i][1] <= want[s2]:
+                    want.pop(s, None)
+                    break
+        for s, v in want.items():
+            QS[q].wait_ge(T.sem[s], v)
+            kn[s] = max(kn.get(s, 0), v)
+        for i in ids:
+            for s, v in toks[i][2].items():
+                kn[s] = max(kn.get(s, 0), v)
+            if toks[i][0][0] != "d":
+                kn[toks[i][0]] = max(kn.get(toks[i][0], 0), toks[i][1])
+
+    def done(q, sem, inc, reads, writes, snap=None):
+        count[sem] = count.get(sem, 0) + inc
+        toks.append((sem, count[sem], dict(known[q]) if snap is None else snap, q))
+        t = len(toks) - 1
+        for r in writes:
+            track(r[0])["w"][cols(r)] = t
+        for r in reads:
+            h = track(r[0])
+            key = q if sem in SEMQ.values() else sem
+            if key not in h["r"]:
+                h["r"][key] = np.full(len(h["w"]), -1)
+            h["r"][key][cols(r)] = t
+
+    def R(name, a=0, b=None, st=1, p=None):
+        if b is None:
+            b = SB[name][0] if name in SB else PS[name]
+        return (name, a, b, st, p)
+
+    def IND(win, off):
+        return ("ind", win, off)
+
+    def ap(r):
+        if r[0] == "ind":
+            return ap(r[1]).indirect(ap(r[2]))
+        n, a, b, st, p = r
+        if n in PLACE:
+            n, at = PLACE[n]
+            a, b = a + at, b + at
+        c = slice(a, b) if st == 1 else slice(a, b, st)
+        return T[n][:, c] if p is None else T[n][0:p, c]
+
+    def flat(rs):
+        out = []
+        for r in rs:
+            if isinstance(r, tuple):
+                if r[0] == "ind":
+                    out += [r[1], r[2]]
+                else:
+                    out.append(r)
+        return out
+
+    def val(s):
+        return ap(s) if isinstance(s, tuple) else s
+
+    def do(q, reads, writes, fn):
+        reads, writes = flat(reads), flat(writes)
+        need(q, reads, writes)
+        fn().then_inc(T.sem[SEMQ[q]], 1)
+        done(q, SEMQ[q], 1, reads, writes)
+
+    def tt(out, a, b, op):
+        do("V", [a, b], [out], lambda: g.vector.tensor_tensor(ap(out), ap(a), ap(b), op))
+
+    def ts(out, a, s1, op0, s2=None, op1=None):
+        if op1 is None:
+            do("V", [a, s1], [out], lambda: g.vector.tensor_scalar(ap(out), ap(a), val(s1), None, op0))
+        else:
+            do("V", [a, s1, s2], [out], lambda: g.vector.tensor_scalar(ap(out), ap(a), val(s1), val(s2), op0, op1))
+
+    def cp(out, a):
+        do("V", [a], [out], lambda: g.vector.tensor_copy(ap(out), ap(a)))
+
+    def scan(out, d0, d1, init, op0, op1):
+        do("V", [d0, d1], [out], lambda: g.vector.tensor_tensor_scan(ap(out), ap(d0), ap(d1), init, op0, op1))
+
+    def act(out, a, f, bias=None, scale=None):
+        def fn():
+            if bias is None and scale is None:
+                return g.scalar.activation(ap(out), ap(a), f)
+            if bias is None:
+                return g.scalar.activation(ap(out), ap(a), f, scale=val(scale))
+            return g.scalar.activation(ap(out), ap(a), f, bias=val(bias), scale=val(scale))
+        do("S", [a, bias, scale], [out], fn)
+
+    def mm(out, l, r, start=True, stop=True):
+        do("T", [l, r], [out], lambda: g.tensor.matmul(ap(out), ap(l), ap(r), start, stop))
+
+    def iota(out, pat, base, cm):
+        if SB[out[0]][1] != I:
+            do("G", [], [out], lambda: g.iota(ap(out), pat, base, cm, allow_small_or_imprecise_dtypes=True))
+        else:
+            do("G", [], [out], lambda: g.iota(ap(out), pat, base, cm))
+
+    nd, nm = [0], [0]
+
+    def newsem():
+        nd[0] += 1
+        return "d%d" % (nd[0] - 1)
+
+    def dma(q, out, in_, reads, writes, sem=None):
+        sem = sem or newsem()
+        need(q, reads, writes)
+        QS[q].dma_start(out, in_).then_inc(T.sem[sem], 16)
+        done(q, sem, 16, reads, writes)
+        return sem
+
+    def send(src, dst, to):
+        k = nm[0]
+        nm[0] += 1
+        engs = topo.engines(core, to)[:8]
+        rid, pid, _s = topo.addr(to)
+        need("G", [src], [])
+        g.remote_dma(out_ap=ap(dst), in_ap=ap(src), remote_sem=T.sem["a%d" % k], local_sem=T.sem["l%d" % k], pid=pid,
+                     routing_id=rid, dma_engine_mask=sum(1 << e for e in engs))
+        done("G", "l%d" % k, len(engs), [src], [])
+        done("G", "a%d" % k, len(engs), [], [dst], {})
+
+    def C(i):
+        return R("col", i, i + 1)
+
+    SH, AN = OP.arith_shift_right, OP.bitwise_and
+    EQ, MU, AD, SU, MX, MN, LE, GT, LT = OP.is_equal, OP.mult, OP.add, OP.subtract, OP.max, OP.min, OP.is_le, OP.is_gt, OP.is_lt
+
+    def expand(zx, z, pieces):
+        w = 256 // pieces
+        for c in range(pieces):
+            act(R(zx, 16 * w * c, 16 * w * c + 16 * w), IND(R(z), R("zl", w * c, w * c + w)), AF.Copy)
+
+    dma("Y", ap(R("vA")), T.v0[:], [], [R("vA")])
+    dma("S", ap(R("zA")), T.z0[:], [], [R("zA")])
+    dma("Y", ap(R("eS")), T.E[:], [], [R("eS")])
+    dma("S", ap(R("LA")), T.L0[:], [], [R("LA")])
+    dma("S", ap(R("xS")), T.X[:], [], [R("xS")])
+    for k in range(3):
+        s = newsem()
+        for gg in range(8):
+            c = R("t%d" % k, 16 * gg, 16 * gg + 16)
+            dma("Y", ap(c), T.E[16 * gg + k, :], [], [c], s)
+    dma("Y", ap(R("e0r")), T.E[0::16, :], [], [R("e0r")])
+    dma("Y", ap(R("e1r")), T.E[1::16, :], [], [R("e1r")])
+
+    iota(R("iC", 0, 1), [[0, 1]], 0, 1)
+    iota(R("iN"), [[1, 256]], 0, 0)
+    iota(R("iD"), [[1, 256]], 128, -1)
+    iota(R("mg"), [[1, 8], [0, 16]], 0, 0)
+    iota(R("gp"), [[0, 2], [1, 8]], 0, 0)
+    iota(R("kk"), [[0, 16], [1, 16]], 0, 0)
+    iota(R("ck"), [[144, 2], [0, 8], [256, 16]], 0, 0)
+    cp(R("vlA"), R("vA"))
+    cp(R("Lo0"), R("LA"))
+    cp(R("zl"), R("iN"))
+    expand("zx0", "zA", 1)
+    send(R("zA"), R("zB"), nxt)
+    send(R("Lo0"), R("LB"), nxt)
+    iota(R("io128"), [[1, 128]], 0, 0)
+    iota(R("g16"), [[0, 2], [16, 8]], 0, 0)
+    iota(R("io16"), [[1, 16]], 0, 0)
+    iota(R("io2k"), [[1, 2048]], 0, 0)
+    ts(R("iC", 1, 2), R("iC", 0, 1), 4, SH)
+    ts(R("iC", 2, 3), R("iC", 0, 1), 15, AN)
+    ts(R("iC", 3, 4), R("iC", 0, 1), 7, AN)
+    ts(R("iC", 4, 5), R("iC", 0, 1), 3, SH, 1, AN)
+    ts(R("iC", 5, 6), R("iC", 0, 1), 3, SH)
+    cp(R("col", 1, 6), R("iC", 1, 6))
+    PG, PK, P7, KY, P8 = C(1), C(2), C(3), C(4), C(5)
+    ts(C(6), PK, 2.0, MU, 1.0, AD)
+    for k in range(4):
+        ts(C(8 + k), PK, float(k), EQ)
+    ts(C(7), C(8), 4096.0, MU)
+    ts(C(12), PK, 2048.0, MU)
+    ts(C(13), PK, 2.0, OP.is_ge)
+    tt(C(20), C(10), C(11), AD)
+    ts(C(14), C(20), -1.0, MU, 1.0, AD)
+    ts(C(15), PK, -2048.0, MU)
+    tt(C(16), C(9), C(8), SU)
+    ts(C(17), KY, -15.0, MU, 16.0, AD)
+    for h in range(2):
+        ts(C(18 + h), PG, float(h), EQ, C(17), MU)
+        ts(C(21 + h), P8, float(h), EQ)
+    ts(C(23), PK, 1.0, AD)
+    act(R("ones"), R("mg"), AF.Identity, 1.0, 0.0)
+    ts(R("If"), R("iD", 0, 128), 128.0, EQ)
+    ts(R("W16"), R("gp"), PG, EQ, 4096.0, MU)
+    ts(R("PHI", 0, 128), R("If"), 0.125, MU)
+    ts(R("PHI", 128, 256), R("If"), -2.0, MU)
+    ts(R("RS01"), R("kk"), 0.0, GT)
+    ts(R("RST"), R("RS01"), -67108864.0, MU, 33554432.0, AD)
+    cp(R("Ib"), R("If"))
+    ts(R("iA"), R("iD"), 15, AN)
+    ts(R("maskJ"), R("iA"), 0.0, EQ)
+    for h in range(2):
+        ts(R("BW%d" % h), R("mg"), P7, EQ, C(18 + h), MU)
+        ts(R("BD%d" % h), R("mg"), P7, EQ, C(21 + h), MU)
+    ts(R("BBf"), R("mg"), PG, EQ)
+    cp(R("BB"), R("BBf"))
+    ts(R("B8p"), R("gp", 0, 8), PG, EQ)
+    ts(R("B8n"), R("gp", 0, 8), PG, EQ, -1.0, MU)
+    ts(R("W8h"), R("gp", 0, 8), PG, EQ, C(6), MU)
+    ts(R("B8f"), R("gp", 0, 8), PG, EQ)
+    ts(R("S8f"), R("gp", 0, 8), PG, EQ, C(8), MU)
+    ts(R("nIb"), R("If"), -1.0, MU)
+    ts(R("Sel0f"), R("BBf"), C(8), MU)
+    ts(R("WY", 0, 8), R("gp", 0, 8), PG, EQ, C(23), MU)
+    ts(R("WY", 8, 16), R("gp", 0, 8), PG, EQ)
+    ts(R("jm"), R("io16"), PK, EQ)
+    for b in range(2):
+        ts(R("P16", 128 * b, 128 * b + 128), R("If"), C(7), MU)
+    for k in range(3):
+        cp(R("tf", 128 * k, 128 * k + 128), R("t%d" % k))
+        mm(R("Q0", 128 * k, 128 * k + 128), R("tf", 128 * k, 128 * k + 128), R("If"))
+    cp(R("elf"), R("Q0", 0, 384))
+    cp(R("el"), R("elf", 0, 256))
+
+    def selectors(part):
+        for j in range(16):
+            c = (128 * j, 128 * j + 128)
+            if part == 0:
+                ts(R("IJ", *c), R("Ib"), R("jm", j, j + 1), MU)
+            else:
+                act(R("BH", *c), R("BB"), AF.Copy, None, R("jm", j, j + 1))
+
+    def tables(el, piece):
+        h, k = piece % 2, piece // 2
+        act(R("XB" if k else "XA", 1024 * h, 1024 * h + 1024), IND(R("xS"), R(el, 128 * k + 64 * h, 128 * k + 64 * h + 64)), AF.Copy)
+
+    def hilo(h):
+        a = (1024 * h, 1024 * h + 1024)
+        tt(R("HI", *a), R("XA", *a), R("XB", *a), MX)
+        tt(R("LO", *a), R("XA", *a), R("XB", *a), MN)
+
+    def yasum(b, bank):
+        mm(R(bank, 0, 512, 1, 16), R("WY"), R("ef", 512 * b, 512 * b + 512))
+        act(R("ys", 512 * b, 512 * b + 512, 1, 16), R(bank, 0, 512, 1, 16), AF.Copy)
+
+    def tolist(bank, out, add, low=False):
+        tt(R("mj"), R(bank, 0, 256), R("maskJ"), MU)
+        scan(R("sc"), R("RS01"), R("mj"), 0.0, MU, AD)
+        if low:
+            cp(R("ui", 0, 16), R("sc", 15, 256, 16))
+            ts(R("ui", 16, 32), R("ui", 0, 16), 2047, AN)
+            cp(R(out), R("ui", 16, 32))
+        else:
+            ts(R(out), R("sc", 15, 256, 16), add, AD)
+
+    def walk(vl, zx, out, marked, sfill, vfill):
+        cp(R("c16"), IND(R("eS"), R(vl)))
+        if not marked and vl == "vlA":
+            cp(R("ef"), R("eS"))
+        act(R("cf"), IND(R("ef"), R(vl)), AF.Copy)
+        act(R("H"), R("cf"), AF.Identity, 1024.0, 0.5)
+        if marked:
+            act(R("mk"), IND(R("MARK"), R(vl)), AF.Copy)
+        for ch in range(4):
+            a = (1024 * ch, 1024 * ch + 1024)
+            tt(R("df", *a), IND(R("xS"), R("c16", 64 * ch, 64 * ch + 64)), R(zx, *a), SU)
+            act(R("ab", *a), R("df", *a), AF.Abs)
+            sfill(ch)
+            if ch % 2 == 1:
+                h = ch // 2
+                kb = "K%d" % h
+                n = (128 * h, 128 * h + 128)
+                mm(R(kb, 0, 256), R("ones", 0, 128, 1, 1), R("ck", 0, 256, 1, 1), True, False)
+                mm(R(kb, 0, 256), R("H", *n), R("PHI"), False, False)
+                mm(R(kb, 128, 256), R("cf", *n), R("If"), False, False)
+                if marked:
+                    mm(R(kb, 0, 256), R("mk", *n), R("P16"), False, False)
+                for k in range(16):
+                    mm(R(kb, k, 256, 16), R("ab", 2048 * h + k, 2048 * h + 2048, 16), R("W16"), False, k == 15)
+        vfill()
+        for h in range(2):
+            scan(R("R", 256 * h, 256 * h + 256), R("RST"), R("K%d" % h, 0, 256), 0.0, MX, MN)
+        ts(R("wi"), R("R", 15, 512, 16), -128.0, AD)
+        ts(R("wa"), R("wi"), 255, AN)
+        cp(R("wb"), R("wa"))
+        mm(R("Q0", 0, 128, 1, 32), R("wb"), R("Ib"))
+        cp(R("wT", 0, 128, 1, 32), R("Q0", 0, 128, 1, 32))
+        for h in range(2):
+            mm(R("N0", 128 * h, 128 * h + 128), R("BW%d" % h, 0, 128, 1, 32), R("wT", 0, 128, 1, 32))
+        tolist("N0", out, -16.0)
+
+    def gapS(L16, zx):
+        e0 = 4096 - 16 * SHARE
+        for tab, sb in (("HI", "sh"), ("LO", "sl")):
+            act(R(sb, 0, 16 * SHARE), IND(R(tab), R(L16, 256 - SHARE, 256)), AF.Copy)
+        i = 0
+        for sb, dst in (("sh", "mh"), ("sl", "ml")):
+            for b in range(SHARE // 32):
+                kb = "K%d" % (i % 2)
+                i += 1
+                mm(R(kb), R("Ib"), R(sb, 512 * b, 512 * b + 512), True, False)
+                mm(R(kb), R("nIb"), R(zx, e0 + 512 * b, e0 + 512 + 512 * b), False, True)
+                act(R(dst, e0 + 512 * b, e0 + 512 + 512 * b), R(kb), AF.Relu)
+
+    def gap(t, L16, zx, h):
+        for c in range(2):
+            n0, n1 = 128 * h + 64 * c, min(128 * h + 64 * c + 64, 256 - SHARE)
+            if n0 < n1:
+                a = (16 * n0, 16 * n1)
+                tt(R("mh", *a), IND(R("HI"), R(L16, n0, n1)), R(zx, *a), MX)
+                tt(R("ml", *a), IND(R("LO"), R(L16, n0, n1)), R(zx, *a), MX)
+        for k in range(16):
+            if k // 2 != t:
+                o = R("G", 128 * h + k, 128 * h + 128, 16)
+                mm(o, R("mh", 2048 * h + k, 2048 * h + 2048, 16), R("B8p"), True, False)
+                mm(o, R("ml", 2048 * h + k, 2048 * h + 2048, 16), R("B8n"), False, True)
+
+    def Q(i):
+        return R("qs", 16 * i, 16 * i + 16)
+
+    def prep(t, z, v1, v2, xi):
+        act(R("r1"), IND(R("io2k"), R(v1)), AF.Copy, None, C(8 + 2 * t))
+        act(R("v2n"), IND(R("io2k"), R(v2)), AF.Copy)
+        act(R("r2"), R("v2n"), AF.Copy, None, C(9 + 2 * t))
+        mm(R("Q0", 0, 256), R("If"), R("Lb"), True, False)
+        mm(R("Q0", 0, 256), R("If"), R("r1"), False, False)
+        mm(R("Q0", 0, 256), R("If"), R("r2"), False, True)
+        act(R("KL"), R("Q0", 0, 256), AF.Copy)
+        mm(R("N1", 0, 256), R("Ib"), R(xi), True, False)
+        mm(R("N1", 0, 256), R("nIb"), R(z), False, True)
+        mm(R("N2", 0, 256), R("Ib"), R(xi), True, False)
+        mm(R("N2", 0, 256), R("Ib"), R(z), False, True)
+
+    def entries(t, z, v1, v2):
+        for e, vl in enumerate((v1, v2)):
+            a = (256 * e, 256 * e + 256)
+            tt(R("eh", *a), IND(R("HI"), R(vl)), R(z), MX)
+            tt(R("en", *a), IND(R("LO"), R(vl)), R(z), MX)
+            for h in range(2):
+                n = (256 * e + 128 * h, 256 * e + 128 * h + 128)
+                o = R("G", 128 * h + 2 * t + e, 128 * h + 128, 16)
+                mm(o, R("eh", *n), R("B8p"), True, False)
+                mm(o, R("en", *n), R("B8n"), False, True)
+
+    def prep2():
+        act(R("ab2"), R("N1", 0, 256), AF.Abs)
+        ts(R("hf"), R("N2", 0, 256), 0.5, MU, -0.25, AD)
+        cp(R("hb"), R("hf"))
+        for h in range(2):
+            n = (128 * h, 128 * h + 128)
+            mm(R("Q1", 8 * h, 8 * h + 8), R("ab2", *n), R("B8p"))
+            mm(R("Q1", 16 + 8 * h, 24 + 8 * h), R("hb", *n), R("W8h"))
+            mm(R("Q1", 32 + 8 * h, 40 + 8 * h), R("v2n", *n), R("S8f"))
+        mm(R("N1", 0, 256), R("BB"), R("ab2"))
+        mm(R("N2", 0, 256), R("Ib"), R("ab2"), True, False)
+        mm(R("N2", 0, 256), R("nIb"), R("hb"), False, True)
+        for h in range(2):
+            mm(R("K0", 128 * h, 128 * h + 128), R("KL", 128 * h, 128 * h + 128), R("If"))
+
+    def prep3(z):
+        ts(Q(0), R("Q1", 0, 16), float(TH), LE, 32768.0, MU)
+        cp(R("qi", 0, 16), R("Q1", 16, 32))
+        cp(Q(1), R("Q1", 32, 48))
+        ts(R("qi", 16, 32), R("qi", 0, 16), 2047, AN)
+        ts(Q(2), Q(0), 0.0, GT)
+        tt(Q(3), Q(1), R("qi", 16, 32), SU)
+        tt(Q(4), Q(3), Q(2), MU)
+        tt(Q(5), Q(4), R("qi", 16, 32), AD)
+        ts(R("like"), R("N1", 0, 256), float(TH), LE)
+        tt(R("tl"), R("N2", 0, 256), R("like"), MU)
+        mm(R("N2", 0, 256), R("Ib"), R(z), True, False)
+        mm(R("N2", 0, 256), R("nIb"), R("hb"), False, False)
+        mm(R("N2", 0, 256), R("nIb"), R("tl"), False, True)
+
+    def onehots(c0, c1):
+        for c in range(c0, c1):
+            ts(R("OH", 256 * c, 256 * c + 128), R("io128"), R("mf", c, c + 1), EQ)
+            ts(R("OH", 256 * c + 128, 256 * c + 256), R("io128"), R("mf", 16 + c, 17 + c), EQ)
+
+    def counts(bank):
+        for c in range(16):
+            mm(R(bank, 0, 128), R("OH", 256 * c, 256 * c + 128), R("OH", 256 * c + 128, 256 * c + 256), c == 0, c == 15)
+
+    def spread(bank):
+        cp(R("kT", 0, 128, 1, 16), R("Q0", 0, 128, 1, 16))
+        for h in range(2):
+            mm(R(bank, 128 * h, 128 * h + 128), R("BD%d" % h, 0, 128, 1, 16), R("kT", 0, 128, 1, 16))
+
+    def decide(t, zo, turned):
+        ts(R("fk"), R("G", 0, 256), float(TAU[t]), LE, 32768.0, MU)
+        tt(R("fk2"), R("K0", 0, 256), R("fk"), AD)
+        scan(R("R2"), R("RST"), R("fk2"), 0.0, MX, MN)
+        tt(Q(6), R("R2", 15, 256, 16), Q(0), MX)
+        mm(R("Q0", 0, 128, 1, 16), Q(6), R("If"))
+        cp(R("mi", 0, 16), Q(6))
+        ts(R("mi", 16, 32), R("mi", 0, 16), 7, SH, 15, AN)
+        ts(R("mi", 32, 48), R("mi", 0, 16), 127, AN)
+        ts(Q(7), Q(6), 32768.0, LT)
+        spread("N0")
+        ts(Q(8), Q(7), -1000.0, MU, 1000.0, AD)
+        tt(Q(9), R("mi", 16, 32), R("g16"), AD)
+        tt(R("mf", 0, 16), Q(9), Q(8), AD)
+        cp(R("mf", 16, 32), R("mi", 32, 48))
+        onehots(0, 5)
+        tolist("N0", "ul", 0.0, True)
+        src = "ce"
+        if turned:
+            act(R("smk"), IND(R("MARK"), R("ul")), AF.Identity, C(8), C(16))
+            cp(R("ce"), IND(R("eS"), R("ul")))
+            ts(R("cutE"), R("N0", 0, 256), 32768.0, LT)
+            tt(R("ce2"), R("ce"), R("smk"), MU)
+            src = "ce2"
+        else:
+            act(R("ce"), IND(R("ef"), R("ul")), AF.Copy)
+            ts(R("cutE"), R("N0", 0, 256), 32768.0, LT)
+        for h in range(2):
+            mm(R("Q1", 48 + 8 * h, 56 + 8 * h), R(src, 128 * h, 128 * h + 128), R("B8f" if turned else "S8f"))
+        tt(R("w"), R("N2", 0, 256), R("cutE"), MU)
+        mm(R("N2", 0, 256), R("Ib"), R("hb"), True, False)
+        mm(R("N2", 0, 256), R("Ib"), R("tl"), False, False)
+        mm(R("N2", 0, 256), R("Ib"), R("w"), False, True)
+        act(R(zo), R("N2", 0, 256), AF.Copy)
+        mm(R("N1", 0, 256), R("BBf" if turned else "Sel0f"), R(src))
+        tt(Q(3), R("Q1", 48, 64), Q(5), SU)
+        tt(Q(4), Q(3), Q(7), MU)
+        tt(R("vo2"), Q(4), Q(5), AD)
+
+    def newlog(Lo):
+        tt(R("oh"), R("N0", 0, 256), R("KL"), EQ)
+        act(R("aK"), R("N1", 0, 256), AF.Identity, C(12), 1.0)
+        tt(R("e1"), R("aK"), R("KL"), SU)
+        tt(R("e2"), R("e1"), R("oh"), MU)
+        tt(R("KL2"), R("KL"), R("e2"), AD)
+        ts(R(Lo), R("KL2"), C(15), AD)
+
+    def turn0():
+        ts(R("m0"), R("Q1", 0, 128), 0.0, GT)
+        for b in range(4):
+            bank = ("N1", "N2")[b % 2]
+            for j in range(4):
+                hi = 4 * b + j
+                mm(R(bank, 128 * j, 128 * j + 128), R("BH", 128 * hi, 128 * hi + 128), R("m0"))
+            act(R("MARK", 512 * b, 512 * b + 512), R(bank), AF.Copy)
+        for j in range(16):
+            mm(R("Q1", 0, 128), R("IJ", 128 * j, 128 * j + 128), R("MARK", j, 2048, 16), j == 0, j == 15)
+
+    def turn1():
+        tt(R("dl"), R("elf", 128, 384), R("elf", 0, 256), SU)
+        cp(R("mlf"), R("Q1", 0, 128))
+        for k in range(2):
+            a = (128 * k, 128 * k + 128)
+            tt(R("dm", *a), R("dl", *a), R("mlf"), MU)
+        tt(R("el2"), R("dm"), R("elf", 0, 256), AD)
+
+    def visit(t, vl, v1, v2, xo, lst, z, L16, ini):
+        def s0(ch):
+            if ch == 0:
+                yasum(2 * t, "N1" if t == 0 else "G")
+            if ch == 1 and t == 1:
+                turn1()
+            if ch == 3:
+                tables(lst, 0)
+                tables(lst, 2)
+
+        def f0():
+            if t == 0:
+                selectors(0)
+
+        def s1(ch):
+            if ch == 0:
+                tables(lst, 1)
+                yasum(2 * t + 1, "N2" if t == 0 else "G")
+            if ch == 1:
+                tables(lst, 3)
+            if ch == 3:
+                expand("zx1", z, 2)
+
+        def f1():
+            hilo(0)
+            hilo(1)
+            ts(R("Lb"), R(L16), C(13 + t), MU, C(12), AD)
+
+        walk(vl, "zx0", v1, t == 1, s0, f0)
+        send(R(v1), R(ini[0]), nxt)
+        walk(v1, "zx0", v2, t == 1, s1, f1)
+        send(R(v2), R(ini[1]), nxt)
+        act(R(xo), IND(R("xS"), R(v2)), AF.Copy)
+        send(R(xo), R(ini[2]), nxt)
+        if t == 1:
+            dma("Y", ap(R("s0r")), T.ys[0:8, :], [R("ys")], [R("s0r")])
+            dma("Y", ap(R("s1r")), T.ys[8:16, :], [R("ys")], [R("s1r")])
+        gapS(L16, "zx1")
+        gap(t, L16, "zx1", 0)
+        prep(t, z, *ini)
+        gap(t, L16, "zx1", 1)
+        prep2()
+        entries(t, z, ini[0], ini[1])
+        if t == 0:
+            selectors(1)
+        prep3(z)
+
+    visit(0, "vlA", "v1o0", "v2o0", "xo0", "el", "zB", "LB", ("v1i0", "v2i0", "xi0"))
+    decide(0, "zo1", False)
+    mm(R("Q0", 0, 128, 1, 16), R("vo2"), R("If"))
+    newlog("Lo1")
+    spread("N0")
+    send(R("zo1"), R("zC"), nxt)
+    send(R("Lo1"), R("LC"), nxt)
+    expand("zx0", "zo1", 4)
+    tolist("N0", "vlB", 0.0)
+    onehots(5, 16)
+    counts("Q1")
+    turn0()
+
+    visit(1, "vlB", "v1o1", "v2o1", "xo1", "el2", "zC", "LC", ("v1i1", "v2i1", "xi1"))
+    decide(1, "zo2", True)
+    send(R("zo2"), R("zF"), home)
+    send(R("vo2"), R("vF"), home)
+    newlog("Lo2")
+    send(R("Lo2"), R("LF"), home)
+    onehots(5, 16)
+    counts("K0")
+    for k in range(2):
+        ts(R("ya1"), R("e%dr" % k), 16.0, MU)
+        tt(R("dy%d" % k), R("ya1"), R("s1r"), SU)
+    ts(R("m1"), R("K0", 0, 128), 0.0, GT)
+    tt(R("ya2"), R("m0"), R("m1"), MX)
+    tt(R("ya3"), R("m0"), R("m1"), MU)
+    tt(R("ya4"), R("ya2"), R("dy0"), MU)
+    tt(R("ya5"), R("ya3"), R("dy1"), MU)
+    tt(R("ya1"), R("ya4"), R("ya5"), AD)
+    tt(R("yas"), R("ya1"), R("s0r"), AD)
+    dma("Y", T.ya[:], ap(R("yas")), [R("yas")], [])
+    act(R("yzs"), R("zF"), AF.Copy)
+    dma("S", T.yz[:], ap(R("yzs")), [R("yzs")], [])
+    mm(R("Q0", 0, 128, 1, 16), R("vF"), R("If"))
+    cp(R("yvs", 0, 128, 1, 16), R("Q0", 0, 128, 1, 16))
+    nv, at = PLACE["yvs"]
+    s = dma("Y", T.yv[:, 0:128], T[nv][0:8, at:at + 128], [R("yvs")], [])
+    dma("Y", T.yv[:, 128:256], T[nv][8:16, at:at + 128], [R("yvs")], [], s)
+    cp(R("yls"), R("LF"))
+    dma("Y", T.yl[:], ap(R("yls")), [R("yls")], [])
+    for s, v in count.items():
+        if known["G"].get(s, 0) < v:
+            g.wait_ge(T.sem[s], v)

@@ -5,23 +5,23 @@ F, B, I, U = "float32", "bfloat16", "int32", "uint16"
 SB = {
     "eS": (2048, I), "xS": (2048, B), "zA": (256, B), "LA": (256, I), "vA": (16, I), "ef": (2048, F),
     "t0": (128, I), "t1": (128, I), "t2": (128, I), "tf": (384, F), "elf": (384, F), "el": (256, U), "el2": (256, U),
-    "e0r": (128, I), "e1r": (128, I), "ys": (2048, F), "s0r": (128, F), "s1r": (128, F), "dy0": (128, F), "dy1": (128, F),
+    "e0r": (128, I), "e1r": (128, I), "ys": (256, F), "s01": (256, F), "dy0": (128, F), "dy1": (128, F),
     "iD": (256, I), "iA": (256, I), "iC": (8, I), "iN": (256, I), "zl": (256, U), "col": (32, F), "mg": (128, F),
     "kk": (256, F), "io128": (128, B), "io16": (16, F), "jm": (16, F), "g16": (16, F), "gp": (16, F), "io2k": (2048, F),
-    "ck": (256, B), "ones": (128, B), "maskJ": (256, F), "Ib": (128, B), "nIb": (128, B), "If": (128, F), "PHI": (256, B),
-    "P16": (256, B), "W16": (16, B), "B8p": (8, B), "B8n": (8, B), "W8h": (8, B), "BB": (128, B), "BBf": (128, F),
-    "Sel0f": (128, F), "S8f": (8, F), "B8f": (8, F), "BW0": (128, B), "BW1": (128, B), "BD0": (128, F), "BD1": (128, F),
-    "BH": (2048, B), "IJ": (2048, B), "RST": (256, F), "RS01": (256, F), "WY": (16, F),
+    "ck": (256, B), "ones": (128, B), "maskJ": (256, F), "Ib": (128, B), "nIb": (128, B), "If": (128, F), "nIf": (128, F),
+    "PHI": (256, B), "P16": (256, B), "W16": (16, B), "B8p": (8, B), "B8n": (8, B), "W8h": (8, B), "BB": (128, B),
+    "BBf": (128, F), "Sel0f": (128, F), "S8f": (8, F), "B8f": (8, F), "BW0": (128, B), "BW1": (128, B), "BD0": (128, F),
+    "BD1": (128, F), "BH": (2048, B), "IJ": (2048, B), "RST": (256, F), "RS01": (256, F), "WY": (16, F),
     "XA": (2048, B), "XB": (2048, B), "HI": (2048, B), "LO": (2048, B), "MARK": (2048, B),
     "zx0": (4096, B), "zx1": (4096, B), "df": (4096, B), "ab": (4096, B), "c16": (256, U), "cf": (256, F), "H": (256, B),
     "mk": (256, B), "R": (512, F), "wi": (32, I), "wa": (32, I), "wb": (32, B), "wT": (128, B), "mj": (256, F),
     "sc": (256, F), "vlA": (16, U), "v1o0": (16, U), "v2o0": (16, U), "v1o1": (16, U), "v2o1": (16, U), "xo0": (256, B),
     "xo1": (256, B), "vlB": (16, U),
     "sh": (1024, B), "sl": (1024, B), "mh": (4096, B), "ml": (4096, B), "eh": (512, B), "en": (512, B), "Lb": (256, F),
-    "r1": (256, F), "r2": (256, F), "v2n": (256, F), "KL": (256, F), "ab2": (256, B), "hf": (256, I), "hb": (256, B),
-    "like": (256, B), "tl": (256, B), "w": (256, B), "fk": (256, F), "fk2": (256, F), "R2": (256, F), "qs": (160, F),
-    "qi": (64, I), "kT": (128, F), "ui": (32, I), "ul": (16, U), "cutE": (256, B), "oh": (256, F), "ce": (256, F),
-    "ce2": (256, F), "smk": (256, F), "aK": (256, F), "e1": (256, F), "e2": (256, F), "KL2": (256, F), "OH": (4096, B),
+    "r1": (256, F), "r2": (256, F), "v2n": (256, F), "KL": (256, F), "Ln": (256, F), "ab2": (256, B), "hf": (256, I),
+    "hb": (256, B), "like": (256, B), "tl": (256, B), "w": (256, B), "fk": (256, F), "fk2": (256, F), "R2": (256, F),
+    "qs": (160, F), "qi": (64, I), "kT": (128, F), "ui": (32, I), "ul": (16, U), "cutE": (256, B), "oh": (256, F),
+    "ce": (256, F), "ce2": (256, F), "smk": (256, F), "e2": (256, F), "KL2": (256, F), "OH": (4096, B),
     "m0": (128, B), "m1": (128, B), "mi": (64, I), "mf": (64, F), "dl": (256, F), "dm": (256, F), "mlf": (128, F),
     "Lo0": (256, U), "zo1": (256, B), "Lo1": (256, U), "zo2": (256, B), "Lo2": (256, U), "vo2": (16, F),
     "zB": (256, B), "LB": (256, U), "v1i0": (16, U), "v2i0": (16, U), "xi0": (256, B), "zC": (256, B), "LC": (256, U),
@@ -230,13 +230,13 @@ def rank_program(g, core, T, topo):
     dma("Y", ap(R("vA")), T.v0[:], [], [R("vA")])
     dma("S", ap(R("zA")), T.z0[:], [], [R("zA")])
     dma("Y", ap(R("eS")), T.E[:], [], [R("eS")])
-    dma("S", ap(R("LA")), T.L0[:], [], [R("LA")])
-    dma("S", ap(R("xS")), T.X[:], [], [R("xS")])
+    dma("Y", ap(R("xS")), T.X[:], [], [R("xS")])
     for k in range(3):
         s = newsem()
         for gg in range(8):
             c = R("t%d" % k, 16 * gg, 16 * gg + 16)
             dma("Y", ap(c), T.E[16 * gg + k, :], [], [c], s)
+    dma("Y", ap(R("LA")), T.L0[:], [], [R("LA")])
     dma("Y", ap(R("e0r")), T.E[0::16, :], [], [R("e0r")])
     dma("Y", ap(R("e1r")), T.E[1::16, :], [], [R("e1r")])
 
@@ -247,12 +247,9 @@ def rank_program(g, core, T, topo):
     iota(R("gp"), [[0, 2], [1, 8]], 0, 0)
     iota(R("kk"), [[0, 16], [1, 16]], 0, 0)
     iota(R("ck"), [[144, 2], [0, 8], [256, 16]], 0, 0)
-    cp(R("vlA"), R("vA"))
-    cp(R("Lo0"), R("LA"))
     cp(R("zl"), R("iN"))
-    expand("zx0", "zA", 1)
+    expand("zx0", "zA", 4)
     send(R("zA"), R("zB"), nxt)
-    send(R("Lo0"), R("LB"), nxt)
     iota(R("io128"), [[1, 128]], 0, 0)
     iota(R("g16"), [[0, 2], [16, 8]], 0, 0)
     iota(R("io16"), [[1, 16]], 0, 0)
@@ -300,17 +297,23 @@ def rank_program(g, core, T, topo):
     ts(R("B8f"), R("gp", 0, 8), PG, EQ)
     ts(R("S8f"), R("gp", 0, 8), PG, EQ, C(8), MU)
     ts(R("nIb"), R("If"), -1.0, MU)
+    ts(R("nIf"), R("If"), -1.0, MU)
     ts(R("Sel0f"), R("BBf"), C(8), MU)
     ts(R("WY", 0, 8), R("gp", 0, 8), PG, EQ, C(23), MU)
     ts(R("WY", 8, 16), R("gp", 0, 8), PG, EQ)
     ts(R("jm"), R("io16"), PK, EQ)
     for b in range(2):
         ts(R("P16", 128 * b, 128 * b + 128), R("If"), C(7), MU)
-    for k in range(3):
-        cp(R("tf", 128 * k, 128 * k + 128), R("t%d" % k))
-        mm(R("Q0", 128 * k, 128 * k + 128), R("tf", 128 * k, 128 * k + 128), R("If"))
-    cp(R("elf"), R("Q0", 0, 384))
-    cp(R("el"), R("elf", 0, 256))
+    cp(R("vlA"), R("vA"))
+
+    def lists(part):
+        if part == 0:
+            for k in range(3):
+                cp(R("tf", 128 * k, 128 * k + 128), R("t%d" % k))
+                mm(R("Q0", 128 * k, 128 * k + 128), R("tf", 128 * k, 128 * k + 128), R("If"))
+        else:
+            cp(R("elf"), R("Q0", 0, 384))
+            cp(R("el"), R("elf", 0, 256))
 
     def selectors(part):
         for j in range(16):
@@ -329,9 +332,14 @@ def rank_program(g, core, T, topo):
         tt(R("HI", *a), R("XA", *a), R("XB", *a), MX)
         tt(R("LO", *a), R("XA", *a), R("XB", *a), MN)
 
-    def yasum(b, bank):
-        mm(R(bank, 0, 512, 1, 16), R("WY"), R("ef", 512 * b, 512 * b + 512))
-        act(R("ys", 512 * b, 512 * b + 512, 1, 16), R(bank, 0, 512, 1, 16), AF.Copy)
+    def yasum(part):
+        if part == 0:
+            for hi in range(16):
+                mm(R("Q1", hi, 256, 16), R("ef", 128 * hi, 128 * hi + 128), R("WY"))
+        else:
+            for b in range(2):
+                mm(R("Q1", 128 * b, 128 * b + 128), R("ys", 128 * b, 128 * b + 128), R("If"))
+        act(R("s01" if part else "ys"), R("Q1", 0, 256), AF.Copy)
 
     def tolist(bank, out, add, low=False):
         tt(R("mj"), R(bank, 0, 256), R("maskJ"), MU)
@@ -345,7 +353,7 @@ def rank_program(g, core, T, topo):
 
     def walk(vl, zx, out, marked, sfill, vfill):
         cp(R("c16"), IND(R("eS"), R(vl)))
-        if not marked and vl == "vlA":
+        if vl == "vlA":
             cp(R("ef"), R("eS"))
         act(R("cf"), IND(R("ef"), R(vl)), AF.Copy)
         act(R("H"), R("cf"), AF.Identity, 1024.0, 0.5)
@@ -385,12 +393,13 @@ def rank_program(g, core, T, topo):
             act(R(sb, 0, 16 * SHARE), IND(R(tab), R(L16, 256 - SHARE, 256)), AF.Copy)
         i = 0
         for sb, dst in (("sh", "mh"), ("sl", "ml")):
-            for b in range(SHARE // 32):
+            for c in range(0, 16 * SHARE, 512):
                 kb = "K%d" % (i % 2)
                 i += 1
-                mm(R(kb), R("Ib"), R(sb, 512 * b, 512 * b + 512), True, False)
-                mm(R(kb), R("nIb"), R(zx, e0 + 512 * b, e0 + 512 + 512 * b), False, True)
-                act(R(dst, e0 + 512 * b, e0 + 512 + 512 * b), R(kb), AF.Relu)
+                w = min(512, 16 * SHARE - c)
+                mm(R(kb, 0, w), R("Ib"), R(sb, c, c + w), True, False)
+                mm(R(kb, 0, w), R("nIb"), R(zx, e0 + c, e0 + c + w), False, True)
+                act(R(dst, e0 + c, e0 + c + w), R(kb, 0, w), AF.Relu)
 
     def gap(t, L16, zx, h):
         for c in range(2):
@@ -416,6 +425,7 @@ def rank_program(g, core, T, topo):
         mm(R("Q0", 0, 256), R("If"), R("r1"), False, False)
         mm(R("Q0", 0, 256), R("If"), R("r2"), False, True)
         act(R("KL"), R("Q0", 0, 256), AF.Copy)
+        act(R("Ln"), R("Q0", 0, 256), AF.Identity, C(15), 1.0)
         mm(R("N1", 0, 256), R("Ib"), R(xi), True, False)
         mm(R("N1", 0, 256), R("nIb"), R(z), False, True)
         mm(R("N2", 0, 256), R("Ib"), R(xi), True, False)
@@ -448,15 +458,15 @@ def rank_program(g, core, T, topo):
             mm(R("K0", 128 * h, 128 * h + 128), R("KL", 128 * h, 128 * h + 128), R("If"))
 
     def prep3(z):
-        ts(Q(0), R("Q1", 0, 16), float(TH), LE, 32768.0, MU)
+        act(Q(0), R("Q1", 0, 16), AF.Relu, 32768.0 * (TH + 1), -32768.0)
+        act(Q(2), Q(0), AF.Sign)
         cp(R("qi", 0, 16), R("Q1", 16, 32))
-        cp(Q(1), R("Q1", 32, 48))
         ts(R("qi", 16, 32), R("qi", 0, 16), 2047, AN)
-        ts(Q(2), Q(0), 0.0, GT)
-        tt(Q(3), Q(1), R("qi", 16, 32), SU)
+        tt(Q(3), R("Q1", 32, 48), R("qi", 16, 32), SU)
         tt(Q(4), Q(3), Q(2), MU)
         tt(Q(5), Q(4), R("qi", 16, 32), AD)
         ts(R("like"), R("N1", 0, 256), float(TH), LE)
+        mm(R("N1", 0, 256), R("nIf"), R("Ln"), True, False)
         tt(R("tl"), R("N2", 0, 256), R("like"), MU)
         mm(R("N2", 0, 256), R("Ib"), R(z), True, False)
         mm(R("N2", 0, 256), R("nIb"), R("hb"), False, False)
@@ -476,7 +486,12 @@ def rank_program(g, core, T, topo):
         for h in range(2):
             mm(R(bank, 128 * h, 128 * h + 128), R("BD%d" % h, 0, 128, 1, 16), R("kT", 0, 128, 1, 16))
 
-    def decide(t, zo, turned):
+    def newlog(Lo):
+        tt(R("e2"), R("N1", 0, 256), R("oh"), MU)
+        tt(R("KL2"), R("Ln"), R("e2"), AD)
+        cp(R(Lo), R("KL2"))
+
+    def decide(t, zo):
         ts(R("fk"), R("G", 0, 256), float(TAU[t]), LE, 32768.0, MU)
         tt(R("fk2"), R("K0", 0, 256), R("fk"), AD)
         scan(R("R2"), R("RST"), R("fk2"), 0.0, MX, MN)
@@ -491,42 +506,38 @@ def rank_program(g, core, T, topo):
         tt(Q(9), R("mi", 16, 32), R("g16"), AD)
         tt(R("mf", 0, 16), Q(9), Q(8), AD)
         cp(R("mf", 16, 32), R("mi", 32, 48))
-        onehots(0, 5)
+        onehots(0, 5 if t == 0 else 2)
         tolist("N0", "ul", 0.0, True)
-        src = "ce"
-        if turned:
+        if t == 1:
             act(R("smk"), IND(R("MARK"), R("ul")), AF.Identity, C(8), C(16))
             cp(R("ce"), IND(R("eS"), R("ul")))
             ts(R("cutE"), R("N0", 0, 256), 32768.0, LT)
             tt(R("ce2"), R("ce"), R("smk"), MU)
-            src = "ce2"
+            mm(R("N1", 0, 256), R("BBf"), R("ce2"), False, True)
         else:
             act(R("ce"), IND(R("ef"), R("ul")), AF.Copy)
             ts(R("cutE"), R("N0", 0, 256), 32768.0, LT)
         for h in range(2):
-            mm(R("Q1", 48 + 8 * h, 56 + 8 * h), R(src, 128 * h, 128 * h + 128), R("B8f" if turned else "S8f"))
+            n = (128 * h, 128 * h + 128)
+            mm(R("Q1", 48 + 8 * h, 56 + 8 * h), R("ce2" if t else "ce", *n), R("B8f" if t else "S8f"))
         tt(R("w"), R("N2", 0, 256), R("cutE"), MU)
+        tt(R("oh"), R("N0", 0, 256), R("KL"), EQ)
+        if t == 0:
+            onehots(5, 8)
         mm(R("N2", 0, 256), R("Ib"), R("hb"), True, False)
         mm(R("N2", 0, 256), R("Ib"), R("tl"), False, False)
         mm(R("N2", 0, 256), R("Ib"), R("w"), False, True)
         act(R(zo), R("N2", 0, 256), AF.Copy)
-        mm(R("N1", 0, 256), R("BBf" if turned else "Sel0f"), R(src))
+        if t == 1:
+            newlog("Lo2")
         tt(Q(3), R("Q1", 48, 64), Q(5), SU)
         tt(Q(4), Q(3), Q(7), MU)
         tt(R("vo2"), Q(4), Q(5), AD)
 
-    def newlog(Lo):
-        tt(R("oh"), R("N0", 0, 256), R("KL"), EQ)
-        act(R("aK"), R("N1", 0, 256), AF.Identity, C(12), 1.0)
-        tt(R("e1"), R("aK"), R("KL"), SU)
-        tt(R("e2"), R("e1"), R("oh"), MU)
-        tt(R("KL2"), R("KL"), R("e2"), AD)
-        ts(R(Lo), R("KL2"), C(15), AD)
-
     def turn0():
         ts(R("m0"), R("Q1", 0, 128), 0.0, GT)
         for b in range(4):
-            bank = ("N1", "N2")[b % 2]
+            bank = ("G", "N2")[b % 2]
             for j in range(4):
                 hi = 4 * b + j
                 mm(R(bank, 128 * j, 128 * j + 128), R("BH", 128 * hi, 128 * hi + 128), R("m0"))
@@ -544,26 +555,33 @@ def rank_program(g, core, T, topo):
 
     def visit(t, vl, v1, v2, xo, lst, z, L16, ini):
         def s0(ch):
-            if ch == 0:
-                yasum(2 * t, "N1" if t == 0 else "G")
-            if ch == 1 and t == 1:
-                turn1()
-            if ch == 3:
-                tables(lst, 0)
-                tables(lst, 2)
+            if t == 0 and ch == 0:
+                yasum(0)
+            if t == 0 and ch == 1:
+                lists(0)
+            if t == 0 and ch == 3:
+                yasum(1)
 
         def f0():
             if t == 0:
+                lists(1)
                 selectors(0)
+                cp(R("Lo0"), R("LA"))
+                send(R("Lo0"), R("LB"), nxt)
+            else:
+                turn1()
+                newlog("Lo1")
+                send(R("Lo1"), R("LC"), nxt)
+            tables(lst, 0)
+            tables(lst, 2)
 
         def s1(ch):
             if ch == 0:
                 tables(lst, 1)
-                yasum(2 * t + 1, "N2" if t == 0 else "G")
             if ch == 1:
                 tables(lst, 3)
             if ch == 3:
-                expand("zx1", z, 2)
+                expand("zx1", z, 4)
 
         def f1():
             hilo(0)
@@ -576,60 +594,55 @@ def rank_program(g, core, T, topo):
         send(R(v2), R(ini[1]), nxt)
         act(R(xo), IND(R("xS"), R(v2)), AF.Copy)
         send(R(xo), R(ini[2]), nxt)
-        if t == 1:
-            dma("Y", ap(R("s0r")), T.ys[0:8, :], [R("ys")], [R("s0r")])
-            dma("Y", ap(R("s1r")), T.ys[8:16, :], [R("ys")], [R("s1r")])
         gapS(L16, "zx1")
         gap(t, L16, "zx1", 0)
         prep(t, z, *ini)
         gap(t, L16, "zx1", 1)
         prep2()
         entries(t, z, ini[0], ini[1])
+        prep3(z)
         if t == 0:
             selectors(1)
-        prep3(z)
 
     visit(0, "vlA", "v1o0", "v2o0", "xo0", "el", "zB", "LB", ("v1i0", "v2i0", "xi0"))
-    decide(0, "zo1", False)
+    decide(0, "zo1")
     mm(R("Q0", 0, 128, 1, 16), R("vo2"), R("If"))
-    newlog("Lo1")
-    spread("N0")
+    spread("K1")
+    mm(R("N1", 0, 256), R("Sel0f"), R("ce"), False, True)
     send(R("zo1"), R("zC"), nxt)
-    send(R("Lo1"), R("LC"), nxt)
     expand("zx0", "zo1", 4)
-    tolist("N0", "vlB", 0.0)
-    onehots(5, 16)
+    tolist("K1", "vlB", 0.0)
+    onehots(8, 16)
     counts("Q1")
     turn0()
 
     visit(1, "vlB", "v1o1", "v2o1", "xo1", "el2", "zC", "LC", ("v1i1", "v2i1", "xi1"))
-    decide(1, "zo2", True)
+    decide(1, "zo2")
     send(R("zo2"), R("zF"), home)
-    send(R("vo2"), R("vF"), home)
-    newlog("Lo2")
     send(R("Lo2"), R("LF"), home)
-    onehots(5, 16)
+    send(R("vo2"), R("vF"), home)
+    onehots(2, 16)
     counts("K0")
     for k in range(2):
         ts(R("ya1"), R("e%dr" % k), 16.0, MU)
-        tt(R("dy%d" % k), R("ya1"), R("s1r"), SU)
+        tt(R("dy%d" % k), R("ya1"), R("s01", 128, 256), SU)
     ts(R("m1"), R("K0", 0, 128), 0.0, GT)
     tt(R("ya2"), R("m0"), R("m1"), MX)
     tt(R("ya3"), R("m0"), R("m1"), MU)
     tt(R("ya4"), R("ya2"), R("dy0"), MU)
     tt(R("ya5"), R("ya3"), R("dy1"), MU)
     tt(R("ya1"), R("ya4"), R("ya5"), AD)
-    tt(R("yas"), R("ya1"), R("s0r"), AD)
+    tt(R("yas"), R("ya1"), R("s01", 0, 128), AD)
     dma("Y", T.ya[:], ap(R("yas")), [R("yas")], [])
     act(R("yzs"), R("zF"), AF.Copy)
     dma("S", T.yz[:], ap(R("yzs")), [R("yzs")], [])
+    cp(R("yls"), R("LF"))
+    dma("Y", T.yl[:], ap(R("yls")), [R("yls")], [])
     mm(R("Q0", 0, 128, 1, 16), R("vF"), R("If"))
     cp(R("yvs", 0, 128, 1, 16), R("Q0", 0, 128, 1, 16))
     nv, at = PLACE["yvs"]
     s = dma("Y", T.yv[:, 0:128], T[nv][0:8, at:at + 128], [R("yvs")], [])
     dma("Y", T.yv[:, 128:256], T[nv][8:16, at:at + 128], [R("yvs")], [], s)
-    cp(R("yls"), R("LF"))
-    dma("Y", T.yl[:], ap(R("yls")), [R("yls")], [])
     for s, v in count.items():
         if known["G"].get(s, 0) < v:
             g.wait_ge(T.sem[s], v)

import numpy as np
from concourse.mybir import AluOpType as OP, AxisListType, ActivationFunctionType as AF

F, B, I, U = "float32", "bfloat16", "int32", "uint16"
SB = {
    "eS": (2048, I), "xS": (2048, B), "zA": (256, B), "LA": (256, I), "vA": (16, I), "ef": (2048, F),
    "t0": (128, I), "t1": (128, I), "t2": (128, I), "tf": (384, F), "elf": (384, F), "el": (256, U), "el2": (256, U),
    "e0r": (128, I), "e1r": (128, I), "ys": (256, F), "s01": (256, F), "dy0": (128, F), "dy1": (128, F),
    "iD": (256, I), "iA": (256, I), "iC": (8, I), "iN": (256, I), "zl": (256, U), "col": (32, F), "mg": (128, F),
    "kk": (256, F), "io128": (128, B), "io16": (16, F), "jm": (16, F), "g16": (16, F), "gp": (16, F), "io2k": (2048, F),
    "ck": (256, B), "ones": (128, B), "maskJ": (256, F), "Ib": (128, B), "nIb": (128, B), "If": (128, F), "nIf": (128, F),
    "PHI": (256, B), "P16": (256, B), "W16": (16, B), "B8p": (8, B), "B8n": (8, B), "W8h": (8, B), "BB": (128, B),
    "BBf": (128, F), "Sel0f": (128, F), "S8f": (8, F), "B8f": (8, F), "BW0": (128, B), "BW1": (128, B), "BD0": (128, F),
    "BD1": (128, F), "BH": (2048, B), "IJ": (2048, B), "RST": (256, F), "RS01": (256, F), "WY": (16, F),
    "XA": (2048, B), "XB": (2048, B), "HI": (2048, B), "LO": (2048, B), "MARK": (2048, B),
    "zx0": (4096, B), "zx1": (4096, B), "df": (4096, B), "ab": (4096, B), "c16": (256, U), "cf": (256, F), "H": (256, B),
    "mk": (256, B), "R": (512, F), "wi": (32, I), "wa": (32, I), "wb": (32, B), "wT": (128, B), "mj": (256, F),
    "sc": (256, F), "vlA": (16, U), "v1o0": (16, U), "v2o0": (16, U), "v1o1": (16, U), "v2o1": (16, U), "xo0": (256, B),
    "xo1": (256, B), "vlB": (16, U),
    "sh": (1024, B), "sl": (1024, B), "mh": (4096, B), "ml": (4096, B), "eh": (512, B), "en": (512, B), "Lb": (256, F),
    "r1": (256, F), "r2": (256, F), "v2n": (256, F), "KL": (256, F), "Ln": (256, F), "ab2": (256, B), "hf": (256, I),
    "hb": (256, B), "like": (256, B), "tl": (256, B), "w": (256, B), "fk": (256, F), "fk2": (256, F), "R2": (256, F),
    "qs": (160, F), "qi": (64, I), "kT": (128, F), "ui": (32, I), "ul": (16, U), "cutE": (256, B), "oh": (256, F),
    "ce": (256, F), "ce2": (256, F), "smk": (256, F), "e2": (256, F), "KL2": (256, F), "OH": (4096, B),
    "m0": (128, B), "m1": (128, B), "mi": (64, I), "mf": (64, F), "dl": (256, F), "dm": (256, F), "mlf": (128, F),
    "Lo0": (256, U), "zo1": (256, B), "Lo1": (256, U), "zo2": (256, B), "Lo2": (256, U), "vo2": (16, F),
    "zB": (256, B), "LB": (256, U), "v1i0": (16, U), "v2i0": (16, U), "xi0": (256, B), "zC": (256, B), "LC": (256, U),
    "v1i1": (16, U), "v2i1": (16, U), "xi1": (256, B), "zF": (256, B), "LF": (256, U), "vF": (16, F),
    "yzs": (256, F), "yls": (256, F), "yvs": (128, F), "yas": (128, F), "ya1": (128, F), "ya2": (128, F), "ya3": (128, F),
    "ya4": (128, F), "ya5": (128, F),
}
PS = {"K0": 512, "K1": 512, "G": 512, "N0": 512, "N1": 512, "N2": 512, "Q0": 512, "Q1": 512}
SCRATCH = {}
PLACE = {}
_use = {F: 0, B: 0, I: 0, U: 0}
for _n, (_w, _d) in SB.items():
    if _w > 600:
        SCRATCH[_n] = ("sbuf", [128, _w], _d)
        PLACE[_n] = (_n, 0)
    else:
        PLACE[_n] = ("all_" + _d, _use[_d])
        _use[_d] += -(-_w // 32) * 32
for _d in _use:
    SCRATCH["all_" + _d] = ("sbuf", [128, _use[_d]], _d)
for _n, _w in PS.items():
    SCRATCH[_n] = ("psum", [128, _w], "float32")
SEMAPHORES = ["cV", "cS", "cT", "cG"] + ["d%d" % i for i in range(30)] + ["a%d" % i for i in range(16)] + ["l%d" % i for i in range(16)]


def rank_program(g, core, T, topo):
    rank = T.rank_of(core)
    if rank is None:
        return
    nR = len(T.cores)
    HOP = 3
    SHARE = 32
    TH, TAU = 1020, (1020, 1530)
    nxt, home = T.cores[(rank + HOP) % nR], T.cores[(rank - 2 * HOP) % nR]

    QS = {"V": g.vector, "S": g.scalar, "T": g.tensor, "G": g, "Y": g.sync}
    SEMQ = {"V": "cV", "S": "cS", "T": "cT", "G": "cG"}
    count = {}
    known = {q: {} for q in QS}
    toks = []
    hist = {}

    def track(name):
        if name not in hist:
            hist[name] = {"w": np.full(SB[name][0] if name in SB else 1, -1), "r": {}}
        return hist[name]

    def cols(r):
        return slice(0, 1) if r[0] in PS else slice(r[1], r[2], r[3])

    def need(q, reads, writes):
        ids = set()
        for r in reads + writes:
            h = track(r[0])
            ps = r[0] in PS
            new = set(int(i) for i in np.unique(h["w"][cols(r)]))
            if ps or r in writes:
                for k, arr in h["r"].items():
                    if not (ps and k == q and r not in writes):
                        new.update(int(i) for i in np.unique(arr[cols(r)]))
            if ps and q == "T":
                new = {i for i in new if i < 0 or toks[i][3] != "T"}
            ids |= new
        ids.discard(-1)
        kn = known[q]
        want = {}
        for i in ids:
            s, v = toks[i][0], toks[i][1]
            if s[0] == "d":
                v = count[s]
            if kn.get(s, 0) < v:
                want[s] = max(want.get(s, 0), v)
        for s in list(want):
            for i in ids:
                s2 = toks[i][0]
                if s2 != s and s2 in want and toks[i][2].get(s, 0) >= want[s] and toks[i][1] <= want[s2]:
                    want.pop(s, None)
                    break
        for s, v in want.items():
            QS[q].wait_ge(T.sem[s], v)
            kn[s] = max(kn.get(s, 0), v)
        for i in ids:
            for s, v in toks[i][2].items():
                kn[s] = max(kn.get(s, 0), v)
            if toks[i][0][0] != "d":
                kn[toks[i][0]] = max(kn.get(toks[i][0], 0), toks[i][1])

    def done(q, sem, inc, reads, writes, snap=None):
        count[sem] = count.get(sem, 0) + inc
        toks.append((sem, count[sem], dict(known[q]) if snap is None else snap, q))
        t = len(toks) - 1
        for r in writes:
            track(r[0])["w"][cols(r)] = t
        for r in reads:
            h = track(r[0])
            key = q if sem in SEMQ.values() else sem
            if key not in h["r"]:
                h["r"][key] = np.full(len(h["w"]), -1)
            h["r"][key][cols(r)] = t

    def R(name, a=0, b=None, st=1, p=None):
        if b is None:
            b = SB[name][0] if name in SB else PS[name]
        return (name, a, b, st, p)

    def IND(win, off):
        return ("ind", win, off)

    def ap(r):
        if r[0] == "ind":
            return ap(r[1]).indirect(ap(r[2]))
        n, a, b, st, p = r
        if n in PLACE:
            n, at = PLACE[n]
            a, b = a + at, b + at
        c = slice(a, b) if st == 1 else slice(a, b, st)
        return T[n][:, c] if p is None else T[n][0:p, c]

    def flat(rs):
        out = []
        for r in rs:
            if isinstance(r, tuple):
                if r[0] == "ind":
                    out += [r[1], r[2]]
                else:
                    out.append(r)
        return out

    def val(s):
        return ap(s) if isinstance(s, tuple) else s

    def do(q, reads, writes, fn):
        reads, writes = flat(reads), flat(writes)
        need(q, reads, writes)
        fn().then_inc(T.sem[SEMQ[q]], 1)
        done(q, SEMQ[q], 1, reads, writes)

    def tt(out, a, b, op):
        do("V", [a, b], [out], lambda: g.vector.tensor_tensor(ap(out), ap(a), ap(b), op))

    def ts(out, a, s1, op0, s2=None, op1=None):
        if op1 is None:
            do("V", [a, s1], [out], lambda: g.vector.tensor_scalar(ap(out), ap(a), val(s1), None, op0))
        else:
            do("V", [a, s1, s2], [out], lambda: g.vector.tensor_scalar(ap(out), ap(a), val(s1), val(s2), op0, op1))

    def cp(out, a):
        do("V", [a], [out], lambda: g.vector.tensor_copy(ap(out), ap(a)))

    def scan(out, d0, d1, init, op0, op1):
        do("V", [d0, d1], [out], lambda: g.vector.tensor_tensor_scan(ap(out), ap(d0), ap(d1), init, op0, op1))

    def act(out, a, f, bias=None, scale=None):
        def fn():
            if bias is None and scale is None:
                return g.scalar.activation(ap(out), ap(a), f)
            if bias is None:
                return g.scalar.activation(ap(out), ap(a), f, scale=val(scale))
            return g.scalar.activation(ap(out), ap(a), f, bias=val(bias), scale=val(scale))
        do("S", [a, bias, scale], [out], fn)

    def mm(out, l, r, start=True, stop=True):
        do("T", [l, r], [out], lambda: g.tensor.matmul(ap(out), ap(l), ap(r), start, stop))

    def iota(out, pat, base, cm):
        if SB[out[0]][1] != I:
            do("G", [], [out], lambda: g.iota(ap(out), pat, base, cm, allow_small_or_imprecise_dtypes=True))
        else:
            do("G", [], [out], lambda: g.iota(ap(out), pat, base, cm))

    nd, nm = [0], [0]

    def newsem():
        nd[0] += 1
        return "d%d" % (nd[0] - 1)

    def dma(q, out, in_, reads, writes, sem=None):
        sem = sem or newsem()
        need(q, reads, writes)
        QS[q].dma_start(out, in_).then_inc(T.sem[sem], 16)
        done(q, sem, 16, reads, writes)
        return sem

    def send(src, dst, to):
        k = nm[0]
        nm[0] += 1
        engs = topo.engines(core, to)[:8]
        rid, pid, _s = topo.addr(to)
        need("G", [src], [])
        g.remote_dma(out_ap=ap(dst), in_ap=ap(src), remote_sem=T.sem["a%d" % k], local_sem=T.sem["l%d" % k], pid=pid,
                     routing_id=rid, dma_engine_mask=sum(1 << e for e in engs))
        done("G", "l%d" % k, len(engs), [src], [])
        done("G", "a%d" % k, len(engs), [], [dst], {})

    def C(i):
        return R("col", i, i + 1)

    SH, AN = OP.arith_shift_right, OP.bitwise_and
    EQ, MU, AD, SU, MX, MN, LE, GT, LT = OP.is_equal, OP.mult, OP.add, OP.subtract, OP.max, OP.min, OP.is_le, OP.is_gt, OP.is_lt

    def expand(zx, z, pieces):
        w = 256 // pieces
        for c in range(pieces):
            act(R(zx, 16 * w * c, 16 * w * c + 16 * w), IND(R(z), R("zl", w * c, w * c + w)), AF.Copy)

    dma("Y", ap(R("vA")), T.v0[:], [], [R("vA")])
    dma("S", ap(R("zA")), T.z0[:], [], [R("zA")])
    dma("Y", ap(R("eS")), T.E[:], [], [R("eS")])
    dma("Y", ap(R("xS")), T.X[:], [], [R("xS")])
    for k in range(3):
        s = newsem()
        for gg in range(8):
            c = R("t%d" % k, 16 * gg, 16 * gg + 16)
            dma("Y", ap(c), T.E[16 * gg + k, :], [], [c], s)
    dma("Y", ap(R("LA")), T.L0[:], [], [R("LA")])
    dma("Y", ap(R("e0r")), T.E[0::16, :], [], [R("e0r")])
    dma("Y", ap(R("e1r")), T.E[1::16, :], [], [R("e1r")])

    iota(R("iC", 0, 1), [[0, 1]], 0, 1)
    iota(R("iN"), [[1, 256]], 0, 0)
    iota(R("iD"), [[1, 256]], 128, -1)
    iota(R("mg"), [[1, 8], [0, 16]], 0, 0)
    iota(R("gp"), [[0, 2], [1, 8]], 0, 0)
    iota(R("kk"), [[0, 16], [1, 16]], 0, 0)
    iota(R("ck"), [[144, 2], [0, 8], [256, 16]], 0, 0)
    cp(R("zl"), R("iN"))
    expand("zx0", "zA", 4)
    send(R("zA"), R("zB"), nxt)
    iota(R("io128"), [[1, 128]], 0, 0)
    iota(R("g16"), [[0, 2], [16, 8]], 0, 0)
    iota(R("io16"), [[1, 16]], 0, 0)
    iota(R("io2k"), [[1, 2048]], 0, 0)
    ts(R("iC", 1, 2), R("iC", 0, 1), 4, SH)
    ts(R("iC", 2, 3), R("iC", 0, 1), 15, AN)
    ts(R("iC", 3, 4), R("iC", 0, 1), 7, AN)
    ts(R("iC", 4, 5), R("iC", 0, 1), 3, SH, 1, AN)
    ts(R("iC", 5, 6), R("iC", 0, 1), 3, SH)
    cp(R("col", 1, 6), R("iC", 1, 6))
    PG, PK, P7, KY, P8 = C(1), C(2), C(3), C(4), C(5)
    ts(C(6), PK, 2.0, MU, 1.0, AD)
    for k in range(4):
        ts(C(8 + k), PK, float(k), EQ)
    ts(C(7), C(8), 4096.0, MU)
    ts(C(12), PK, 2048.0, MU)
    ts(C(13), PK, 2.0, OP.is_ge)
    tt(C(20), C(10), C(11), AD)
    ts(C(14), C(20), -1.0, MU, 1.0, AD)
    ts(C(15), PK, -2048.0, MU)
    tt(C(16), C(9), C(8), SU)
    ts(C(17), KY, -15.0, MU, 16.0, AD)
    for h in range(2):
        ts(C(18 + h), PG, float(h), EQ, C(17), MU)
        ts(C(21 + h), P8, float(h), EQ)
    ts(C(23), PK, 1.0, AD)
    act(R("ones"), R("mg"), AF.Identity, 1.0, 0.0)
    ts(R("If"), R("iD", 0, 128), 128.0, EQ)
    ts(R("W16"), R("gp"), PG, EQ, 4096.0, MU)
    ts(R("PHI", 0, 128), R("If"), 0.125, MU)
    ts(R("PHI", 128, 256), R("If"), -2.0, MU)
    ts(R("RS01"), R("kk"), 0.0, GT)
    ts(R("RST"), R("RS01"), -67108864.0, MU, 33554432.0, AD)
    cp(R("Ib"), R("If"))
    ts(R("iA"), R("iD"), 15, AN)
    ts(R("maskJ"), R("iA"), 0.0, EQ)
    for h in range(2):
        ts(R("BW%d" % h), R("mg"), P7, EQ, C(18 + h), MU)
        ts(R("BD%d" % h), R("mg"), P7, EQ, C(21 + h), MU)
    ts(R("BBf"), R("mg"), PG, EQ)
    cp(R("BB"), R("BBf"))
    ts(R("B8p"), R("gp", 0, 8), PG, EQ)
    ts(R("B8n"), R("gp", 0, 8), PG, EQ, -1.0, MU)
    ts(R("W8h"), R("gp", 0, 8), PG, EQ, C(6), MU)
    ts(R("B8f"), R("gp", 0, 8), PG, EQ)
    ts(R("S8f"), R("gp", 0, 8), PG, EQ, C(8), MU)
    ts(R("nIb"), R("If"), -1.0, MU)
    ts(R("nIf"), R("If"), -1.0, MU)
    ts(R("Sel0f"), R("BBf"), C(8), MU)
    ts(R("WY", 0, 8), R("gp", 0, 8), PG, EQ, C(23), MU)
    ts(R("WY", 8, 16), R("gp", 0, 8), PG, EQ)
    ts(R("jm"), R("io16"), PK, EQ)
    for b in range(2):
        ts(R("P16", 128 * b, 128 * b + 128), R("If"), C(7), MU)
    cp(R("vlA"), R("vA"))

    def lists(part):
        if part == 0:
            for k in range(3):
                cp(R("tf", 128 * k, 128 * k + 128), R("t%d" % k))
                mm(R("Q0", 128 * k, 128 * k + 128), R("tf", 128 * k, 128 * k + 128), R("If"))
        else:
            cp(R("elf"), R("Q0", 0, 384))
            cp(R("el"), R("elf", 0, 256))

    def selectors(part):
        for j in range(16):
            c = (128 * j, 128 * j + 128)
            if part == 0:
                ts(R("IJ", *c), R("Ib"), R("jm", j, j + 1), MU)
            else:
                act(R("BH", *c), R("BB"), AF.Copy, None, R("jm", j, j + 1))

    def tables(el, piece):
        h, k = piece % 2, piece // 2
        act(R("XB" if k else "XA", 1024 * h, 1024 * h + 1024), IND(R("xS"), R(el, 128 * k + 64 * h, 128 * k + 64 * h + 64)), AF.Copy)

    def hilo(h):
        a = (1024 * h, 1024 * h + 1024)
        tt(R("HI", *a), R("XA", *a), R("XB", *a), MX)
        tt(R("LO", *a), R("XA", *a), R("XB", *a), MN)

    def yasum(part):
        if part == 0:
            for hi in range(16):
                mm(R("Q1", hi, 256, 16), R("ef", 128 * hi, 128 * hi + 128), R("WY"))
        else:
            for b in range(2):
                mm(R("Q1", 128 * b, 128 * b + 128), R("ys", 128 * b, 128 * b + 128), R("If"))
        act(R("s01" if part else "ys"), R("Q1", 0, 256), AF.Copy)

    def tolist(bank, out, add, low=False):
        tt(R("mj"), R(bank, 0, 256), R("maskJ"), MU)
        scan(R("sc"), R("RS01"), R("mj"), 0.0, MU, AD)
        if low:
            cp(R("ui", 0, 16), R("sc", 15, 256, 16))
            ts(R("ui", 16, 32), R("ui", 0, 16), 2047, AN)
            cp(R(out), R("ui", 16, 32))
        else:
            ts(R(out), R("sc", 15, 256, 16), add, AD)

    def walk(vl, zx, out, marked, sfill, vfill):
        cp(R("c16"), IND(R("eS"), R(vl)))
        if vl == "vlA":
            cp(R("ef"), R("eS"))
        act(R("cf"), IND(R("ef"), R(vl)), AF.Copy)
        act(R("H"), R("cf"), AF.Identity, 1024.0, 0.5)
        if marked:
            act(R("mk"), IND(R("MARK"), R(vl)), AF.Copy)
        for ch in range(4):
            a = (1024 * ch, 1024 * ch + 1024)
            tt(R("df", *a), IND(R("xS"), R("c16", 64 * ch, 64 * ch + 64)), R(zx, *a), SU)
            act(R("ab", *a), R("df", *a), AF.Abs)
            sfill(ch)
            if ch % 2 == 1:
                h = ch // 2
                kb = "K%d" % h
                n = (128 * h, 128 * h + 128)
                mm(R(kb, 0, 256), R("ones", 0, 128, 1, 1), R("ck", 0, 256, 1, 1), True, False)
                mm(R(kb, 0, 256), R("H", *n), R("PHI"), False, False)
                mm(R(kb, 128, 256), R("cf", *n), R("If"), False, False)
                if marked:
                    mm(R(kb, 0, 256), R("mk", *n), R("P16"), False, False)
                for k in range(16):
                    mm(R(kb, k, 256, 16), R("ab", 2048 * h + k, 2048 * h + 2048, 16), R("W16"), False, k == 15)
        vfill()
        for h in range(2):
            scan(R("R", 256 * h, 256 * h + 256), R("RST"), R("K%d" % h, 0, 256), 0.0, MX, MN)
        ts(R("wi"), R("R", 15, 512, 16), -128.0, AD)
        ts(R("wa"), R("wi"), 255, AN)
        cp(R("wb"), R("wa"))
        mm(R("Q0", 0, 128, 1, 32), R("wb"), R("Ib"))
        cp(R("wT", 0, 128, 1, 32), R("Q0", 0, 128, 1, 32))
        for h in range(2):
            mm(R("N0", 128 * h, 128 * h + 128), R("BW%d" % h, 0, 128, 1, 32), R("wT", 0, 128, 1, 32))
        tolist("N0", out, -16.0)

    def gapS(L16, zx):
        e0 = 4096 - 16 * SHARE
        for tab, sb in (("HI", "sh"), ("LO", "sl")):
            act(R(sb, 0, 16 * SHARE), IND(R(tab), R(L16, 256 - SHARE, 256)), AF.Copy)
        i = 0
        for sb, dst in (("sh", "mh"), ("sl", "ml")):
            for c in range(0, 16 * SHARE, 512):
                kb = "K%d" % (i % 2)
                i += 1
                w = min(512, 16 * SHARE - c)
                mm(R(kb, 0, w), R("Ib"), R(sb, c, c + w), True, False)
                mm(R(kb, 0, w), R("nIb"), R(zx, e0 + c, e0 + c + w), False, True)
                act(R(dst, e0 + c, e0 + c + w), R(kb, 0, w), AF.Relu)

    def gap(t, L16, zx, h):
        for c in range(2):
            n0, n1 = 128 * h + 64 * c, min(128 * h + 64 * c + 64, 256 - SHARE)
            if n0 < n1:
                a = (16 * n0, 16 * n1)
                tt(R("mh", *a), IND(R("HI"), R(L16, n0, n1)), R(zx, *a), MX)
                tt(R("ml", *a), IND(R("LO"), R(L16, n0, n1)), R(zx, *a), MX)
        for k in range(16):
            if k // 2 != t:
                o = R("G", 128 * h + k, 128 * h + 128, 16)
                mm(o, R("mh", 2048 * h + k, 2048 * h + 2048, 16), R("B8p"), True, False)
                mm(o, R("ml", 2048 * h + k, 2048 * h + 2048, 16), R("B8n"), False, True)

    def Q(i):
        return R("qs", 16 * i, 16 * i + 16)

    def prep(t, z, v1, v2, xi):
        act(R("r1"), IND(R("io2k"), R(v1)), AF.Copy, None, C(8 + 2 * t))
        act(R("v2n"), IND(R("io2k"), R(v2)), AF.Copy)
        act(R("r2"), R("v2n"), AF.Copy, None, C(9 + 2 * t))
        mm(R("Q0", 0, 256), R("If"), R("Lb"), True, False)
        mm(R("Q0", 0, 256), R("If"), R("r1"), False, False)
        mm(R("Q0", 0, 256), R("If"), R("r2"), False, True)
        act(R("KL"), R("Q0", 0, 256), AF.Copy)
        act(R("Ln"), R("Q0", 0, 256), AF.Identity, C(15), 1.0)
        mm(R("N1", 0, 256), R("Ib"), R(xi), True, False)
        mm(R("N1", 0, 256), R("nIb"), R(z), False, True)
        mm(R("N2", 0, 256), R("Ib"), R(xi), True, False)
        mm(R("N2", 0, 256), R("Ib"), R(z), False, True)

    def entries(t, z, v1, v2):
        for e, vl in enumerate((v1, v2)):
            a = (256 * e, 256 * e + 256)
            tt(R("eh", *a), IND(R("HI"), R(vl)), R(z), MX)
            tt(R("en", *a), IND(R("LO"), R(vl)), R(z), MX)
            for h in range(2):
                n = (256 * e + 128 * h, 256 * e + 128 * h + 128)
                o = R("G", 128 * h + 2 * t + e, 128 * h + 128, 16)
                mm(o, R("eh", *n), R("B8p"), True, False)
                mm(o, R("en", *n), R("B8n"), False, True)

    def prep2():
        act(R("ab2"), R("N1", 0, 256), AF.Abs)
        ts(R("hf"), R("N2", 0, 256), 0.5, MU, -0.25, AD)
        cp(R("hb"), R("hf"))
        for h in range(2):
            n = (128 * h, 128 * h + 128)
            mm(R("Q1", 8 * h, 8 * h + 8), R("ab2", *n), R("B8p"))
            mm(R("Q1", 16 + 8 * h, 24 + 8 * h), R("hb", *n), R("W8h"))
            mm(R("Q1", 32 + 8 * h, 40 + 8 * h), R("v2n", *n), R("S8f"))
        mm(R("N1", 0, 256), R("BB"), R("ab2"))
        mm(R("N2", 0, 256), R("Ib"), R("ab2"), True, False)
        mm(R("N2", 0, 256), R("nIb"), R("hb"), False, True)
        for h in range(2):
            mm(R("K0", 128 * h, 128 * h + 128), R("KL", 128 * h, 128 * h + 128), R("If"))

    def prep3(z):
        act(Q(0), R("Q1", 0, 16), AF.Relu, 32768.0 * (TH + 1), -32768.0)
        act(Q(2), Q(0), AF.Sign)
        cp(R("qi", 0, 16), R("Q1", 16, 32))
        ts(R("qi", 16, 32), R("qi", 0, 16), 2047, AN)
        tt(Q(3), R("Q1", 32, 48), R("qi", 16, 32), SU)
        tt(Q(4), Q(3), Q(2), MU)
        tt(Q(5), Q(4), R("qi", 16, 32), AD)
        ts(R("like"), R("N1", 0, 256), float(TH), LE)
        mm(R("N1", 0, 256), R("nIf"), R("Ln"), True, False)
        tt(R("tl"), R("N2", 0, 256), R("like"), MU)
        mm(R("N2", 0, 256), R("Ib"), R(z), True, False)
        mm(R("N2", 0, 256), R("nIb"), R("hb"), False, False)
        mm(R("N2", 0, 256), R("nIb"), R("tl"), False, True)

    def onehots(c0, c1):
        for c in range(c0, c1):
            ts(R("OH", 256 * c, 256 * c + 128), R("io128"), R("mf", c, c + 1), EQ)
            ts(R("OH", 256 * c + 128, 256 * c + 256), R("io128"), R("mf", 16 + c, 17 + c), EQ)

    def counts(bank):
        for c in range(16):
            mm(R(bank, 0, 128), R("OH", 256 * c, 256 * c + 128), R("OH", 256 * c + 128, 256 * c + 256), c == 0, c == 15)

    def spread(bank):
        cp(R("kT", 0, 128, 1, 16), R("Q0", 0, 128, 1, 16))
        for h in range(2):
            mm(R(bank, 128 * h, 128 * h + 128), R("BD%d" % h, 0, 128, 1, 16), R("kT", 0, 128, 1, 16))

    def newlog(Lo):
        tt(R("e2"), R("N1", 0, 256), R("oh"), MU)
        tt(R("KL2"), R("Ln"), R("e2"), AD)
        cp(R(Lo), R("KL2"))

    def decide(t, zo):
        ts(R("fk"), R("G", 0, 256), float(TAU[t]), LE, 32768.0, MU)
        tt(R("fk2"), R("K0", 0, 256), R("fk"), AD)
        scan(R("R2"), R("RST"), R("fk2"), 0.0, MX, MN)
        tt(Q(6), R("R2", 15, 256, 16), Q(0), MX)
        mm(R("Q0", 0, 128, 1, 16), Q(6), R("If"))
        cp(R("mi", 0, 16), Q(6))
        ts(R("mi", 16, 32), R("mi", 0, 16), 7, SH, 15, AN)
        ts(R("mi", 32, 48), R("mi", 0, 16), 127, AN)
        ts(Q(7), Q(6), 32768.0, LT)
        spread("N0")
        ts(Q(8), Q(7), -1000.0, MU, 1000.0, AD)
        tt(Q(9), R("mi", 16, 32), R("g16"), AD)
        tt(R("mf", 0, 16), Q(9), Q(8), AD)
        cp(R("mf", 16, 32), R("mi", 32, 48))
        onehots(0, 5 if t == 0 else 2)
        tolist("N0", "ul", 0.0, True)
        if t == 1:
            act(R("smk"), IND(R("MARK"), R("ul")), AF.Identity, C(8), C(16))
            cp(R("ce"), IND(R("eS"), R("ul")))
            ts(R("cutE"), R("N0", 0, 256), 32768.0, LT)
            tt(R("ce2"), R("ce"), R("smk"), MU)
            mm(R("N1", 0, 256), R("BBf"), R("ce2"), False, True)
        else:
            act(R("ce"), IND(R("ef"), R("ul")), AF.Copy)
            ts(R("cutE"), R("N0", 0, 256), 32768.0, LT)
        for h in range(2):
            n = (128 * h, 128 * h + 128)
            mm(R("Q1", 48 + 8 * h, 56 + 8 * h), R("ce2" if t else "ce", *n), R("B8f" if t else "S8f"))
        tt(R("w"), R("N2", 0, 256), R("cutE"), MU)
        tt(R("oh"), R("N0", 0, 256), R("KL"), EQ)
        if t == 0:
            onehots(5, 8)
        mm(R("N2", 0, 256), R("Ib"), R("hb"), True, False)
        mm(R("N2", 0, 256), R("Ib"), R("tl"), False, False)
        mm(R("N2", 0, 256), R("Ib"), R("w"), False, True)
        act(R(zo), R("N2", 0, 256), AF.Copy)
        if t == 1:
            newlog("Lo2")
        tt(Q(3), R("Q1", 48, 64), Q(5), SU)
        tt(Q(4), Q(3), Q(7), MU)
        tt(R("vo2"), Q(4), Q(5), AD)

    def turn0():
        ts(R("m0"), R("Q1", 0, 128), 0.0, GT)
        for b in range(4):
            bank = ("G", "N2")[b % 2]
            for j in range(4):
                hi = 4 * b + j
                mm(R(bank, 128 * j, 128 * j + 128), R("BH", 128 * hi, 128 * hi + 128), R("m0"))
            act(R("MARK", 512 * b, 512 * b + 512), R(bank), AF.Copy)
        for j in range(16):
            mm(R("Q1", 0, 128), R("IJ", 128 * j, 128 * j + 128), R("MARK", j, 2048, 16), j == 0, j == 15)

    def turn1():
        tt(R("dl"), R("elf", 128, 384), R("elf", 0, 256), SU)
        cp(R("mlf"), R("Q1", 0, 128))
        for k in range(2):
            a = (128 * k, 128 * k + 128)
            tt(R("dm", *a), R("dl", *a), R("mlf"), MU)
        tt(R("el2"), R("dm"), R("elf", 0, 256), AD)

    def visit(t, vl, v1, v2, xo, lst, z, L16, ini):
        def s0(ch):
            if t == 0 and ch == 0:
                yasum(0)
            if t == 0 and ch == 1:
                lists(0)
            if t == 0 and ch == 3:
                yasum(1)

        def f0():
            if t == 0:
                lists(1)
                selectors(0)
                cp(R("Lo0"), R("LA"))
                send(R("Lo0"), R("LB"), nxt)
            else:
                turn1()
                newlog("Lo1")
                send(R("Lo1"), R("LC"), nxt)
            tables(lst, 0)
            tables(lst, 2)

        def s1(ch):
            if ch == 0:
                tables(lst, 1)
            if ch == 1:
                tables(lst, 3)
            if ch == 3:
                expand("zx1", z, 4)

        def f1():
            hilo(0)
            hilo(1)
            ts(R("Lb"), R(L16), C(13 + t), MU, C(12), AD)

        walk(vl, "zx0", v1, t == 1, s0, f0)
        send(R(v1), R(ini[0]), nxt)
        walk(v1, "zx0", v2, t == 1, s1, f1)
        send(R(v2), R(ini[1]), nxt)
        act(R(xo), IND(R("xS"), R(v2)), AF.Copy)
        send(R(xo), R(ini[2]), nxt)
        gapS(L16, "zx1")
        gap(t, L16, "zx1", 0)
        prep(t, z, *ini)
        gap(t, L16, "zx1", 1)
        prep2()
        entries(t, z, ini[0], ini[1])
        prep3(z)
        if t == 0:
            selectors(1)

    visit(0, "vlA", "v1o0", "v2o0", "xo0", "el", "zB", "LB", ("v1i0", "v2i0", "xi0"))
    decide(0, "zo1")
    mm(R("Q0", 0, 128, 1, 16), R("vo2"), R("If"))
    spread("K1")
    mm(R("N1", 0, 256), R("Sel0f"), R("ce"), False, True)
    send(R("zo1"), R("zC"), nxt)
    expand("zx0", "zo1", 4)
    tolist("K1", "vlB", 0.0)
    onehots(8, 16)
    counts("Q1")
    turn0()

    visit(1, "vlB", "v1o1", "v2o1", "xo1", "el2", "zC", "LC", ("v1i1", "v2i1", "xi1"))
    decide(1, "zo2")
    send(R("zo2"), R("zF"), home)
    send(R("Lo2"), R("LF"), home)
    send(R("vo2"), R("vF"), home)
    onehots(2, 16)
    counts("K0")
    for k in range(2):
        ts(R("ya1"), R("e%dr" % k), 16.0, MU)
        tt(R("dy%d" % k), R("ya1"), R("s01", 128, 256), SU)
    ts(R("m1"), R("K0", 0, 128), 0.0, GT)
    tt(R("ya2"), R("m0"), R("m1"), MX)
    tt(R("ya3"), R("m0"), R("m1"), MU)
    tt(R("ya4"), R("ya2"), R("dy0"), MU)
    tt(R("ya5"), R("ya3"), R("dy1"), MU)
    tt(R("ya1"), R("ya4"), R("ya5"), AD)
    tt(R("yas"), R("ya1"), R("s01", 0, 128), AD)
    dma("Y", T.ya[:], ap(R("yas")), [R("yas")], [])
    act(R("yzs"), R("zF"), AF.Copy)
    dma("S", T.yz[:], ap(R("yzs")), [R("yzs")], [])
    cp(R("yls"), R("LF"))
    dma("Y", T.yl[:], ap(R("yls")), [R("yls")], [])
    mm(R("Q0", 0, 128, 1, 16), R("vF"), R("If"))
    cp(R("yvs", 0, 128, 1, 16), R("Q0", 0, 128, 1, 16))
    nv, at = PLACE["yvs"]
    s = dma("Y", T.yv[:, 0:128], T[nv][0:8, at:at + 128], [R("yvs")], [])
    dma("Y", T.yv[:, 128:256], T[nv][8:16, at:at + 128], [R("yvs")], [], s)
    for s, v in count.items():
        if known["G"].get(s, 0) < v:
            g.wait_ge(T.sem[s], v)
